import numpy as np, ml_dtypes
CORES = [24,25,26,27,28,29,30,31]
N = 8
import mx_ref
BF = ml_dtypes.bfloat16
def gcols(t, e):
    v = np.concatenate([t.reshape(8, 16, -1, 4), np.zeros((8, 16, 1, 4), BF)], axis=2)
    return np.ascontiguousarray(np.stack([v[g][:, e[g]] for g in range(8)])).reshape(128, -1)
def tile(rs):
    return np.stack(rs, axis=2).reshape(128, -1).astype(BF)
def cut(t, i, w=512):
    return t[:, w * i:w * i + w]
def pick(q, e):
    c = np.concatenate([q[0].reshape(128, -1, 4), np.zeros((128, 1, 4), np.uint8)], axis=1); s = np.concatenate([q[1], np.ones((16, 1), np.uint8)], axis=1)
    return (np.ascontiguousarray(c[:, e].reshape(128, -1)), np.ascontiguousarray(s[:, e]))
def join(*qs):
    return (np.concatenate([q[0] for q in qs], axis=1), np.concatenate([q[1] for q in qs], axis=1))
def put(q, e, v):
    c, s = q[0].reshape(128, -1, 4).copy(), q[1].copy(); c[:, e] = v[0].reshape(128, -1, 4); s[:, e] = v[1]
    return (c.reshape(128, -1), s)
def pk(c, s):
    return (np.ascontiguousarray(c), mx_ref.live(s))
def emit(q):
    return q[0], q[1]
def packed(v, rng):
    q = [mx_ref.quantize(np.ascontiguousarray(v[r])) for r in range(N)]
    return np.stack([a for a, b in q]), np.stack([mx_ref.plane(b, rng) for a, b in q])
def values_of_codes():
    e, c = np.zeros((128, 128, 4), np.float32), np.zeros((128, 2, 4), np.uint8)
    e[np.arange(128), np.arange(128), 0] = 1
    c[:127, :, 0] = np.arange(256).reshape(2, 128).T[:127]
    return mx_ref.matmul(mx_ref.quantize(e.reshape(128, 512).astype(BF)), (c.reshape(128, 8), np.full((16, 2), 127, np.uint8))).T.reshape(-1).astype(np.float64)
CODE_VALUE, SCALE_VALUE = values_of_codes(), 2.0 ** (np.arange(256) - 127.0)
def decode(q):
    return (CODE_VALUE[q[0]].reshape(16, 8, -1, 4) * SCALE_VALUE[q[1]][:, None, :, None] + 0.0).reshape(128, -1).astype(np.float32)
def f(rng, *shape):
    return mx_ref.flush((rng.standard_normal(shape, dtype=np.float32) * np.exp2(rng.integers(-2, 3, shape[:-1] + (1,)))).astype(BF))
def wide(rng, *shape, cols=0):
    v = rng.standard_normal(shape, dtype=np.float32) * np.exp2(rng.integers(-12, 13, shape)).astype(np.float32)
    if cols: v *= np.repeat(np.exp2(rng.integers(-cols, cols + 1, shape[:-2] + (1, shape[-1] // 4))) * (rng.random(shape[:-2] + (1, shape[-1] // 4)) > 0.0625), 4, axis=-1).astype(np.float32)
    return mx_ref.flush(v.astype(BF))
C, L1, H1, L2, H2, K, R = 256, 96, 160, 64, 80, 96, 3
def big(v):
    v = v.astype(np.float32)
    v[np.abs(v) < np.float32(2.0 ** -16)] = 0
    return v.astype(BF)
def numbers_of(rng):
    return {"x": big(f(rng, N, 128, 4 * C)), "u": np.array(f(rng, N, 128, 512)), "v": np.array(f(rng, N, 128, 512))}
def layers(rng):
    return big(f(rng, N, 128, 2048)).reshape(N, 8, 16, 4, 8, 16, 4)
def weights(rng, w):
    c, p = packed(np.ascontiguousarray(w).reshape(N, 128, 2048), rng)
    return {"wc": c, "ws": p}
def setup_inputs(rng):
    return {**numbers_of(rng), **weights(rng, layers(rng))}
def setup_inputs_ties(rng):
    d = numbers_of(rng)
    x = d["x"].reshape(N, 8, 16, C, 4)
    x[:, :, 0] = 0
    x[:, :, 0, :, :2] = np.where(rng.random((N, 8, C, 2)) < 0.125, 3, rng.integers(1, 3, (N, 8, C, 2))).astype(np.float32).astype(BF)
    u = d["u"].reshape(N, 128, 128, 4)
    u[:, :, ::16] = 0
    u[:, :, 1::16] = 0
    e = int(rng.integers(N))
    k = rng.permutation(N - 2) % 2 * 2.0 - 1.0
    for i in range(N - 2):
        r = (e + 1 + i) % N
        for h in range(0, 128, 16):
            u[r, h, h, 0] = k[i]
            u[r, h, h + 1, 1] = k[i]
    w = layers(rng)
    w[:, :, :, :, :, 0] = 0
    return {"x": x.reshape(N, 128, 4 * C), "u": u.reshape(N, 128, 512), "v": d["v"], **weights(rng, w)}
def setup_inputs_near(rng):
    d = numbers_of(rng)
    x = d["x"].astype(np.float32).reshape(N, 8, 16, C, 4)
    x[:, :, 0] = 0
    x[:, :, 8:] = 0
    u = d["u"].reshape(N, 128, 128, 4)
    u[:, :, ::16] = 0
    u[:, :, 1::16] = 0
    o = rng.permutation(N) % 4
    for r in range(N):
        k = 1.0 if o[r] == 0 else 2.0 ** -30
        if o[r] < 3:
            s = rng.integers(0, 16, (8, C))
            x[r, :, 8] = ((s[:, :, None] >> np.arange(4)) & 1) * np.exp2(np.arange(4) - 23.0)
        if o[r] < 2:
            x[r, :, 0, :, 0] = 1.0 - 2.0 * o[r]
            x[r, :, 11, :, 0] = 2.0 ** -10
        if o[r] == 2: x[r, :, 0, :, 0] = -1.0 * (rng.random((8, C)) < 0.25)
        if o[r] == 3:
            s = rng.random((8, C)) < 0.25
            x[r, :, 10, :, 0] = np.where(s, 9.0, 0.0) * 2.0 ** -32
            x[r, :, 12, :, 0] = np.where(s, 0.0, 8.0) * 2.0 ** -32
        for h in range(0, 128, 16):
            for i in (h, h + 1):
                u[r, h, i, 0] = 1.0 if o[r] == 2 else k
                u[r, h + 8, i] = k
                u[r, h + 10, i, 0] = k * 1.125
                u[r, h + 11, i, 0] = k
                u[r, h + 12, i, 0] = k * 1.25
    w = layers(rng)
    w[:, :, :, :, :, 0] = 0
    w[:, :, :, :, :, 8:] = 0
    return {"x": x.reshape(N, 128, 4 * C).astype(BF), "u": u.reshape(N, 128, 512), "v": d["v"], **weights(rng, w)}
def setup_inputs_huge(rng):
    d = numbers_of(rng)
    e = rng.permutation(N)
    x = -0.6 - 0.4 * rng.random((N, 8, 16, C, 4))
    a = 0.9 + 0.1 * rng.random((N, 128, 128, 4))
    x[e[0], :, :15] = -1.0
    for i in (L1 - 1, H1 + 1): x[e[0], :, :, i] = -0.625
    a[e[0]] = 1.0
    u = d["u"].astype(np.float32).reshape(N, 128, 128, 4)
    for r in range(N):
        both = r in e[1::2]
        if both: x[r] *= rng.choice([-1.0, 1.0], (8, 1, C, 1))
        for h in range(0, 128, 16):
            i = slice(h, h + 16) if both else slice(0, 128)
            u[r, :, h:h + 2] = 0
            u[r, i, h:h + 2] = 2.0 ** 30 * a[r, i, h:h + 2]
    w = np.zeros((N, 128, 4, 128, 4), np.float32)
    i = np.arange(128)
    for b in range(4): w[:, i, b, i, b] = -1
    return {"x": (2.0 ** 30 * x).astype(np.float32).reshape(N, 128, 4 * C).astype(BF), "u": u.astype(BF).reshape(N, 128, 512), "v": d["v"], **weights(rng, w.astype(BF))}
def setup_inputs_edge(rng):
    d = numbers_of(rng)
    x = d["x"].reshape(N, 8, 16, C, 4)
    c = np.where(rng.random((N, 8)) < 0.25, rng.integers(L1, H1 + 1, (N, 8)), rng.choice([L1, H1], (N, 8)))
    k = np.where(rng.random((N, 8)) < 0.25, rng.integers(L2, H2 + 1, (N, 8)), rng.choice([L2, H2], (N, 8)))
    e = int(rng.integers(N))
    for r in (e, (e + 1) % N):
        c[r] = H1
        k[r] = L2
    x[:, :, 0] = 0
    x[:, :, 0, :, :2] = rng.integers(-1, 2, (N, 8, C, 2)).astype(np.float32).astype(BF)
    for i in (L1 - 1, H1 + 1): x[:, :, 0, i, 0] = 4.0
    for i in (L2 - 1, H2 + 1): x[:, :, 0, i, 1] = 4.0
    for r in range(N):
        for g in range(8):
            x[r, g, 0, c[r, g], 0] = 2.0
            x[r, g, 0, k[r, g], 1] = 2.0
    n = (N, 8, 8, C, 4)
    s = np.exp2(-1.0 * rng.integers(8, 15, n)) * (1.0 + (2 * rng.integers(0, 64, n) + 1) * 2.0 ** -7) * rng.choice([-1.0, 1.0], n)
    s[:, :, 0, :, 0] = 1.96875 * rng.choice([-1.0, 1.0], (N, 8, C))
    x[:, :, 8:] = s.astype(np.float32).astype(BF)
    u = d["u"].reshape(N, 128, 128, 4)
    u[:, :, ::16] = 0
    u[:, :, 1::16] = 0
    for h in range(0, 128, 16):
        u[:, h, h, 0] = 1
        u[:, h, h + 1, 1] = 1
    return {"x": x.reshape(N, 128, 4 * C), "u": u.reshape(N, 128, 512), "v": d["v"], **weights(rng, layers(rng))}
def setup_inputs_spread(rng):
    d = setup_inputs(rng)
    d["x"] = big(wide(rng, N, 128, 4 * C, cols=6))
    return d
def check_inputs(d):
    b = []
    for k in ("x", "u", "v"):
        a = np.abs(d[k].astype(np.float32))
        if not (np.isfinite(a).all() and ((a == 0) | (a >= 2.0 ** -30) & (a <= 2.0 ** 30)).all()): b.append("a value of " + k)
    none, least, most = [emit(mx_ref.quantize(np.full((128, 16), k, np.float32).astype(BF)))[1][0, 0] for k in (0.0, 2.0 ** -30, 2.0 ** 30)]
    for r in range(N):
        if ((d["wc"][r] == 0x7F) | (d["wc"][r] == 0xFF)).any(): b.append("wc: a code that is no number")
        s = mx_ref.live(d["ws"][r])
        if ((s != none) & ((s < least) | (s > most))).any(): b.append("ws: a scale out of range")
    return b
def folded(c, k):
    p = np.arange(C)
    q = np.where(p < c, c - 1 - p, p - c)
    z = np.where(q < k, k - 1 - q, q - k)
    right = (p >= c).astype(np.int64)
    leaf = np.where(q < k, right, 3 - right)
    o = np.argsort(4 * z + leaf, axis=1)
    zo = np.take_along_axis(z, o, axis=1)
    first = np.ones((8, C), bool)
    first[:, 1:] = zo[:, 1:] != zo[:, :-1]
    low, above = np.full((8, K), -1), C + z
    g, j = np.nonzero(first)
    low[g, zo[g, j]] = o[g, j]
    g, j = np.nonzero(~first)
    above[g, o[g, j - 1]] = o[g, j]
    return o, low, above
def reference(x, u, v, wc, ws):
    qu = [mx_ref.quantize(u[r]) for r in range(N)]
    lay = [pk(wc[r], ws[r]) for r in range(N)]
    now = [x[r] for r in range(N)]
    for t in range(R):
        own, folds, sent = [], [], []
        for r in range(N):
            q = mx_ref.quantize(now[r])
            own.append(decode(q))
            s = mx_ref.matmul(qu[r], q) + np.float32(0.0)
            c = L1 + np.argmax(s[::16, L1:H1 + 1], axis=1)
            k = L2 + np.argmax(s[1::16, L2:H2 + 1], axis=1)
            folds.append(folded(c[:, None], k[:, None]))
            sent.append(mx_ref.quantize(gcols(now[r], folds[r][1])))
        came = decode(join(*sent)).astype(BF)
        for r in range(N):
            o, low, above = folds[r]
            a = np.concatenate([own[r].astype(BF), cut(came, (r + 1) % N, 4 * K)], axis=1)
            z = mx_ref.quantize(((own[r] + gcols(a, above).astype(np.float32)) * np.float32(0.5)).astype(BF))
            made = tile([mx_ref.matmul(pick(lay[r], np.arange(128 * b, 128 * b + 128)), z) * np.float32(0.03125) + own[r][:, b::4] for b in range(4)])
            now[r] = gcols(made, o)
    y, lo = np.zeros((N, 128, C), np.float32), np.zeros((N, 8, C), np.float32)
    oc, osc = np.zeros((N, 128, 4 * C), np.uint8), np.zeros((N, 16, C), np.uint8)
    for r in range(N):
        q = mx_ref.quantize(now[r])
        y[r] = mx_ref.matmul(mx_ref.quantize(v[r]), q)
        lo[r] = folds[r][0]
        oc[r], osc[r] = emit(q)
    return {"y": y, "lo": lo, "oc": oc, "osc": osc}

@@ -1,0 +1,395 @@
+from concourse.mybir import dt, AluOpType as A, AxisListType, ActivationFunctionType as F
+
+R, C, K = 3, 256, 96
+PAD = 80
+XWID = 4 * (C + 2 * PAD)
+XB = 4 * PAD
+AWID = C + K
+
+WORK = {}
+_n = [0]
+for _name, _w in (("NEG", 72), ("PC", 72), ("PK", 24), ("MC", 72), ("MK", 24), ("C4", 1), ("K4", 1), ("S15", 1), ("T3", 1),
+                  ("QT", 1), ("J", 16), ("J1", 16), ("J3", 16), ("H1", 16), ("J2A", 16), ("J2B", 16), ("I1", 16), ("ZQ", 8),
+                  ("mk", 8), ("hb", 8), ("f", 1), ("b1", 8), ("a1", 8), ("q", 8), ("r0", 8), ("r", 8),
+                  ("c", 1), ("k", 1), ("n3", 1), ("n2", 1), ("cpk", 1), ("k2", 1), ("c2", 1), ("tau", 1), ("st2", 1),
+                  ("w1", 1), ("w0", 1), ("rho", 1), ("th3", 1), ("a", 1),
+                  ("s1", 16), ("s2", 16), ("s3", 16), ("s4", 16), ("e1", 16), ("e2", 16), ("e3", 16), ("e4", 16), ("e5", 16),
+                  ("g1", 16), ("g2", 16), ("g3", 16), ("h1", 16), ("h2", 16), ("h3", 16), ("h4", 16), ("h5", 16), ("h6", 16),
+                  ("l2", 16), ("l3", 16), ("l4", 16), ("m1", 16), ("m2", 16), ("t1", 16), ("t2", 16), ("t3", 16), ("u", 16),
+                  ("N", 16), ("i", 16), ("q1", 16), ("I", 16), ("mo", 16), ("zn", 16), ("x1", 16), ("lf", 16), ("lg", 16),
+                  ("gg", 16), ("km", 16), ("zk", 16), ("D", 16), ("gD", 16)):
+    WORK[_name] = (_n[0], _w)
+    _n[0] += -(-_w // 8) * 8
+
+SCRATCH = {
+    "wk": ("sbuf", [128, _n[0]], "float32"),
+    "IP": ("sbuf", [128, 1], "int32"), "M16": ("sbuf", [128, 16], "int32"), "UI": ("sbuf", [128, 16], "int32"),
+    "I15": ("sbuf", [128, 1], "int32"), "I3": ("sbuf", [128, 1], "int32"), "ZI": ("sbuf", [128, 16], "int32"),
+    "PLACE": ("sbuf", [128, C], "float32"), "LOF": ("sbuf", [128, C], "float32"), "YO": ("sbuf", [128, C], "float32"),
+    "UO": ("sbuf", [128, 16], "uint16"), "LB1": ("sbuf", [128, 16], "uint16"), "LB2": ("sbuf", [128, 8], "uint16"),
+    "LC": ("sbuf", [128, 16], "uint16"), "LO": ("sbuf", [128, 16], "uint16"),
+    "ONE": ("sbuf", [128, 516], "bfloat16"), "EB": ("sbuf", [128, 516], "bfloat16"),
+    "UT": ("sbuf", [128, 512], "bfloat16"), "VT": ("sbuf", [128, 512], "bfloat16"), "BT": ("sbuf", [128, 512], "bfloat16"),
+    "ZT": ("sbuf", [128, 4 * C], "bfloat16"), "YS": ("sbuf", [128, 4 * C], "bfloat16"), "AW": ("sbuf", [128, 4 * AWID], "bfloat16"),
+    "FH": ("sbuf", [128, 4 * C], "bfloat16"),
+}
+for _name, _w in (("E", 512), ("QU", 128), ("UC", 256), ("QV", 128), ("W", 512), ("QZ", 256), ("QM0", 128), ("QM1", 128), ("QM2", 128),
+                  ("QX0", AWID), ("QX1", AWID), ("QX2", AWID), ("QX3", C), ("QB0", 128), ("QB1", 128), ("QB2", 128)):
+    SCRATCH[_name + "c"] = ("sbuf", [128, _w], "float8_e4m3fn_x4")
+    SCRATCH[_name + "p"] = ("sbuf", [128, _w], "uint8")
+for _t in range(R + 1):
+    SCRATCH["XW%d" % _t] = ("sbuf", [128, XWID], "bfloat16")
+for _b in range(8):
+    SCRATCH["p%d" % _b] = ("psum", [128, 512], "float32")
+LOADS = ["xm", "xa", "xb", "u", "v", "wc", "ws"]
+STORES = ["oc", "os0", "os1", "os2", "os3", "y0", "y1", "lo"]
+SEMAPHORES = ["cv", "cs", "ct", "cg"] + ["d_" + n for n in LOADS + STORES] + ["arr%d" % t for t in range(R)] + ["loc%d" % t for t in range(R)]
+
+
+def rank_program(g, core, T, topo):
+    rank = T.rank_of(core)
+    if rank is None:
+        return
+    V, S, P, Y = g.vector, g.scalar, g.tensor, g.sync
+    queue = {"v": V, "s": S, "t": P, "g": g, "y": Y}
+    count = {}
+    waited = {}
+    known = {q: {} for q in queue}
+    behind = {}
+    log = {}
+
+    def need(q, name, a, b, write, out):
+        for x in log.get(name, ()):
+            if x[0] < b and a < x[1]:
+                if x[3] != q:
+                    if write or x[2] or name[0] == "p" and name[1:].isdigit():
+                        out.append(x[4])
+                elif x[2] and not write:
+                    out.append(x[4])
+
+    def note(q, name, a, b, write, ev):
+        rows = log.setdefault(name, [])
+        if write:
+            rows[:] = [x for x in rows if not (a <= x[0] and x[1] <= b)]
+        rows.append((a, b, write, q, ev))
+
+    def wait(q, ev):
+        sem, val = ev
+        if known[q].get(sem, 0) >= val:
+            return
+        queue[q].wait_ge(T.sem[sem], val)
+        waited[sem] = max(waited.get(sem, 0), val)
+        for s, n in list(behind.get(ev, {}).items()) + [(sem, val)]:
+            known[q][s] = max(known[q].get(s, 0), n)
+
+    def pre(q, rd, wr):
+        evs = []
+        for r in rd:
+            need(q, r[0], r[1], r[2], False, evs)
+        for r in wr:
+            need(q, r[0], r[1], r[2], True, evs)
+        most = {}
+        for s, n in evs:
+            most[s] = max(most.get(s, 0), n)
+        for s in sorted(most, key=lambda s: (s == "c" + q, s)):
+            wait(q, (s, most[s]))
+
+    def emit(q, fn, rd, wr):
+        pre(q, rd, wr)
+        sem = "c" + q
+        count[sem] = count.get(sem, 0) + 1
+        fn().then_inc(T.sem[sem], 1)
+        ev = (sem, count[sem])
+        behind[ev] = dict(known[q])
+        for r in rd:
+            note(q, r[0], r[1], r[2], False, ev)
+        for r in wr:
+            note(q, r[0], r[1], r[2], True, ev)
+
+    def dma(q, name, out, in_, rd, wr):
+        pre(q, rd, wr)
+        sem = "d_" + name
+        count[sem] = 16
+        queue[q].dma_start(out, in_).then_inc(T.sem[sem], 16)
+        ev = (sem, 16)
+        behind[ev] = dict(known[q])
+        for r in rd:
+            note(sem, r[0], r[1], r[2], False, ev)
+        for r in wr:
+            note(sem, r[0], r[1], r[2], True, ev)
+
+    def reg(n):
+        return ("wk", WORK[n][0], WORK[n][0] + WORK[n][1])
+
+    def cut(n, a, b):
+        return ("wk", WORK[n][0] + a, WORK[n][0] + b)
+
+    def norm(x):
+        return reg(x) if isinstance(x, str) else x
+
+    def ap(x):
+        return T[x[0]][:, x[1]:x[2]]
+
+    def lanes(name, a, b):
+        return [(name + "#%d" % i, a, b) for i in range(4)]
+
+    def ts(out, in0, s1, s2, op0, op1=None, wr=None, oap=None):
+        out, in0 = (norm(out) if out is not None else None), norm(in0)
+        rd = [in0]
+        sc = []
+        for s in (s1, s2):
+            if isinstance(s, (str, tuple)):
+                s = norm(s)
+                rd.append(s)
+                s = ap(s)
+            sc.append(s)
+        o = ap(out) if oap is None else oap
+        if op1 is None:
+            emit("v", lambda: V.tensor_scalar(o, ap(in0), sc[0], None, op0), rd, wr or [out])
+        else:
+            emit("v", lambda: V.tensor_scalar(o, ap(in0), sc[0], sc[1], op0, op1), rd, wr or [out])
+
+    def tt(out, x, y, op):
+        out, x, y = norm(out), norm(x), norm(y)
+        emit("v", lambda: V.tensor_tensor(ap(out), ap(x), ap(y), op), [x, y], [out])
+
+    def ident(out, x, scale, bias):
+        out, x = norm(out), norm(x)
+        rd = [x]
+        if isinstance(bias, str):
+            bias = norm(bias)
+            rd.append(bias)
+            bias = ap(bias)
+        emit("s", lambda: S.activation(ap(out), ap(x), F.Identity, bias=bias, scale=scale), rd, [out])
+
+    def quant(dst, a, n, src, sa, rd):
+        emit("v", lambda: V.quantize_mx(T[dst + "c"][:, a:a + n], T[dst + "p"][:, a:a + n], T[src][:, sa:sa + 4 * n]), rd, [(dst, a, a + n)])
+
+    def mm(bank, n, st, sa, mv, ma, start=True, stop=True):
+        emit("t", lambda: P.matmul_mx(T["p%d" % bank][:, 0:n], T[st + "c"][:, sa:sa + 128], T[st + "p"][:, sa:sa + 128],
+                                      T[mv + "c"][:, ma:ma + n], T[mv + "p"][:, ma:ma + n], start, stop),
+             [(st, sa, sa + 128), (mv, ma, ma + n)], [("p%d" % bank, 0, 512)])
+
+    def fill(name, a, b, val, wr=None):
+        emit("v", lambda: V.memset(T[name][:, a:b], val), [], wr or [(name, a, b)])
+
+    def psum_copy(q, out, wr, bank, a, b, scale):
+        rd = [("p%d" % bank, 0, 512)]
+        src = T["p%d" % bank][:, a:b]
+        if q == "v":
+            emit("v", lambda: V.tensor_scalar(out, src, scale, None, A.mult), rd, [wr])
+        else:
+            emit("s", lambda: S.activation(out, src, F.Copy, scale=scale), rd, [wr])
+
+    def gather(q, out, win, off, rd, wr):
+        if q == "v":
+            emit("v", lambda: V.tensor_copy(out, win.indirect(off)), rd, wr)
+        else:
+            emit("s", lambda: S.activation(out, win.indirect(off), F.Copy), rd, wr)
+
+    for name, a, b in (("xm", 64, 192), ("xa", 0, 64), ("xb", 192, 256)):
+        dma("y", name, T.XW0[:, XB + 4 * a:XB + 4 * b], T.x[:, 4 * a:4 * b], [], lanes("XW0", a, b))
+    dma("s", "u", T.UT[:, 0:512], T.u[:, 0:512], [], [("UT", 0, 512)])
+    dma("y", "wc", T.Wc[:, 0:512].bitcast(dt.uint8), T.wc[:, 0:2048], [], [("W", 0, 512)])
+    dma("y", "ws", T.Wp[:, 0:512], T.ws[:, 0:512], [], [("Ws", 0, 512)])
+    dma("y", "v", T.VT[:, 0:512], T.v[:, 0:512], [], [("VT", 0, 512)])
+
+    fill("ONE", 0, 516, 32.0)
+    emit("g", lambda: g.iota(T.UI[:, 0:16], [[1, 2], [16, 8]], 0, 0), [], [("UI", 0, 16)])
+    emit("g", lambda: g.iota(T.IP[:, 0:1], [[1, 1]], 0, 1), [], [("IP", 0, 1)])
+    emit("g", lambda: g.iota(T.M16[:, 0:16], [[16, 16]], 0, 0), [], [("M16", 0, 16)])
+    emit("g", lambda: g.affine_select(T.EB[:, 0:516], T.ONE[:, 0:516], [[-1, 516]], A.is_equal, 0.0, 4, 4), [("ONE", 0, 516)], [("EB", 0, 516)])
+    emit("g", lambda: g.iota(T.PLACE[:, 0:C], [[1, C]], 0, 0, allow_small_or_imprecise_dtypes=True), [], [("PLACE", 0, C)])
+    fill("wk", WORK["NEG"][0], WORK["NEG"][0] + 72, -1.0e29)
+    fill("wk", WORK["MK"][0] + 17, WORK["MK"][0] + 18, 256.0)
+    fill("BT", 384, 512, 0.0, lanes("BT", 96, 128))
+    emit("v", lambda: V.tensor_copy(T.UO[:, 0:16], T.UI[:, 0:16]), [("UI", 0, 16)], [("UO", 0, 16)])
+    ts(("I15", 0, 1), ("IP", 0, 1), 15, None, A.bitwise_and)
+    ts(("I3", 0, 1), ("IP", 0, 1), 3, None, A.bitwise_and)
+    fill("XW0", 0, XB, 0.0, lanes("XW0", -PAD, 0))
+    emit("v", lambda: V.tensor_copy(ap(reg("S15")), T.I15[:, 0:1]), [("I15", 0, 1)], [reg("S15")])
+    emit("v", lambda: V.tensor_copy(ap(reg("T3")), T.I3[:, 0:1]), [("I3", 0, 1)], [reg("T3")])
+    fill("XW0", XB + 4 * C, XWID, 0.0, lanes("XW0", C, C + PAD))
+    ts("J", ("M16", 0, 16), "S15", None, A.add)
+    ts(cut("MC", 65, 66), "T3", 382.0, None, A.add)
+    ts("QT", "T3", -0.25, 0.5, A.mult, A.add)
+    ts("I1", "J", "T3", 322.0, A.subtract, A.add)
+    ts("ZQ", cut("J", 0, 8), "T3", 258.0, A.subtract, A.add)
+    quant("QU", 0, 128, "UT", 0, [("UT", 0, 512)])
+    emit("s", lambda: S.activation(T.UCp[:, 0:256], T.QUp[:, 0:128].indirect(T.UO[:, 0:16]), F.Copy), [("QU", 0, 128), ("UO", 0, 16)], [("UCs", 0, 256)])
+    emit("v", lambda: V.tensor_copy(T.UCc[:, 0:256].bitcast(dt.uint32), T.QUc[:, 0:128].bitcast(dt.uint32).indirect(T.UO[:, 0:16])),
+         [("QU", 0, 128), ("UO", 0, 16)], [("UC", 0, 256)])
+
+    dst = T.cores[(rank - 1) % len(T.cores)]
+    rid, pid = topo.addr(dst)[:2]
+    mask = topo.mask(core, dst)
+    lands = 2 * len(topo.engines(core, dst))
+    order = [2, 3, 0, 1]
+
+    for t in range(R):
+        last = t == R - 1
+        XW, QX, QM, QB = "XW%d" % t, "QX%d" % t, "QM%d" % t, "QB%d" % t
+        NX = "XW%d" % (t + 1)
+        quant(QM, 0, 128, XW, XB + 4 * 64, lanes(XW, 64, 192))
+        if t == 0:
+            pre("t", [("UCs", 0, 256)], [])
+        mm(5, 128, "UC", 128, QM, 0)
+        mm(4, 128, "UC", 0, QM, 0)
+        if t > 0:
+            for a in (0, 192):
+                gather("v", T[XW][:, XB + 4 * a:XB + 4 * a + 256:4], T.YS[:, 0:C], T.LO[:, a // 16:a // 16 + 4],
+                       [("YS", 0, C), ("LO", 0, 16)], [(XW + "#0", a, a + 64)])
+        emit("v", lambda: V.tensor_tensor_scan(ap(cut("PK", 0, 17)), T.p5[:, 0:17], ap(cut("NEG", 0, 17)), -1.0e29, A.max, A.max),
+             [("p5", 0, 512), reg("NEG")], [cut("PK", 0, 17)])
+        emit("v", lambda: V.tensor_tensor_scan(ap(cut("PC", 0, 65)), T.p4[:, 32:97], ap(cut("NEG", 0, 65)), -1.0e29, A.max, A.max),
+             [("p4", 0, 512), reg("NEG")], [cut("PC", 0, 65)])
+        ts(cut("MK", 0, 17), cut("PK", 0, 17), cut("PK", 16, 17), 4.0, A.is_lt, A.mult)
+        ts(cut("MC", 0, 65), cut("PC", 0, 65), cut("PC", 64, 65), 4.0, A.is_lt, A.mult)
+        emit("v", lambda: V.tensor_reduce(ap(reg("K4")), ap(cut("MK", 0, 18)), AxisListType.X, A.add), [cut("MK", 0, 18)], [reg("K4")])
+        emit("v", lambda: V.tensor_reduce(ap(reg("C4")), ap(cut("MC", 0, 66)), AxisListType.X, A.add), [cut("MC", 0, 66)], [reg("C4")])
+        ts("mk", "ZQ", "K4", None, A.is_gt)
+        ts(None, "I1", "C4", "K4", A.add, A.subtract, wr=[("LB1", 0, 16)], oap=T.LB1[:, 0:16])
+        ts("hb", "ZQ", "K4", None, A.add)
+        ts("f", "K4", 2.0, "C4", A.mult, A.is_lt)
+        tt("b1", "hb", "mk", A.mult)
+        ts("a1", "ZQ", "K4", 0.0, A.subtract, A.min)
+        ts("q", "b1", "f", -2.0, A.mult, A.mult)
+        tt("r0", "a1", "b1", A.add)
+        tt("r", "r0", "q", A.add)
+        ts(None, "r", "C4", float(XB), A.add, A.add, wr=[("LB2", 0, 8)], oap=T.LB2[:, 0:8])
+        allx = lanes(XW, -PAD, C + PAD)
+        gather("s", T.BT[:, 0:256], T[XW][:, 0:XWID], T.LB1[:, 0:16], allx + [("LB1", 0, 16)], lanes("BT", 0, 64))
+        gather("v", T.BT[:, 256:384], T[XW][:, 0:XWID], T.LB2[:, 0:8], allx + [("LB2", 0, 8)], lanes("BT", 64, 96))
+        quant(QB, 0, 128, "BT", 0, lanes("BT", 0, 128))
+        pre("g", [(QB, 0, 96)], [])
+        g.remote_dma(out_ap=T[QX + "c"][:, C:AWID].bitcast(dt.uint8), in_ap=T[QB + "c"][:, 0:K].bitcast(dt.uint8),
+                     remote_sem=T.sem["arr%d" % t], local_sem=T.sem["loc%d" % t], pid=pid, routing_id=rid, dma_engine_mask=mask)
+        g.remote_dma(out_ap=T[QX + "p"][:, C:AWID], in_ap=T[QB + "p"][:, 0:K],
+                     remote_sem=T.sem["arr%d" % t], local_sem=T.sem["loc%d" % t], pid=pid, routing_id=rid, dma_engine_mask=mask)
+        count["arr%d" % t] = lands
+        count["loc%d" % t] = lands
+        note("remote", QX, C, AWID, True, ("arr%d" % t, lands))
+        quant(QX, 0, C, XW, XB, lanes(XW, 0, C))
+        if t == 0:
+            for b in range(4):
+                quant("E", 128 * b, 128, "EB", 4 - b, [("EB", 0, 516)])
+        for b in range(4):
+            mm(b, C, "E", 128 * b, QX, 0)
+        for b in order:
+            mm(4 + b, C, "E", 128 * b, QX, 0, True, False)
+        ident("c", "C4", 0.25, "QT")
+        ident("k", "K4", 0.25, 0.0)
+        ident("k2", "K4", 0.5, 0.0)
+        ident("cpk", "K4", 0.25, "c")
+        ident("n3", "K4", -0.25, "c")
+        ident("c2", "c", 2.0, 0.0)
+        ident("n2", "cpk", -1.0, 256.0)
+        ident("tau", "cpk", 2.0, -256.0)
+        ident("w1", "k2", 1.0, "cpk")
+        ident("w0", "c2", 1.0, "cpk")
+        ident("st2", "k2", 1.0, "n2")
+        for b in range(4):
+            psum_copy("s", T.AW[:, AWID * b:AWID * b + C], ("AW", AWID * b, AWID * b + C), b, 0, C, 1.0 / 64)
+            psum_copy("s", T.FH[:, C * b:C * b + C], ("FH", C * b, C * b + C), b, 0, C, 1.0 / 64)
+        if t == 0:
+            ts("J1", "J", -1.0, None, A.add)
+            ts("J3", "J", -256.5, None, A.add)
+            ts("H1", "J", 0.25, -0.375, A.mult, A.add)
+            ts("J2A", "J", 2.0, -255.0, A.mult, A.add)
+            ts("J2B", "J", 2.0, 257.0, A.mult, A.add)
+        ts("rho", "k2", "c", None, A.max)
+        ts("th3", "tau", "c", None, A.max)
+        ts("s1", "J", "n3", "n2", A.is_ge, A.mult)
+        ts("s2", "J", "c", "st2", A.is_ge, A.mult)
+        ts("s3", "J", "th3", "n2", A.is_ge, A.mult)
+        ts("s4", "J", "cpk", "k2", A.is_ge, A.mult)
+        ts("e1", "J", "tau", None, A.is_lt)
+        ts("e2", "J2A", "w1", None, A.subtract)
+        ts("e3", "J", "rho", None, A.is_ge)
+        ts("g1", "J", "c2", None, A.is_ge)
+        ts("g2", "J2B", "w0", None, A.subtract)
+        tt("h1", "s2", "s1", A.subtract)
+        tt("h2", "s3", "s4", A.add)
+        tt("e4", "e1", "e2", A.mult)
+        tt("g3", "g1", "g2", A.mult)
+        tt("h3", "h1", "h2", A.subtract)
+        tt("e5", "e4", "e3", A.mult)
+        tt("h4", "g3", "J", A.subtract)
+        ts("a", "n2", "n3", None, A.min)
+        tt("h5", "e5", "h3", A.add)
+        ts("l3", "J3", "k2", 0.5, A.add, A.mult)
+        ts("l2", "J1", "a", 1.0 / 3, A.subtract, A.mult)
+        tt("h6", "h5", "h4", A.add)
+        ts("l4", "J", "k2", "a", A.subtract, A.subtract)
+        ts(None, "h6", "n3", 255.0, A.add, A.add, wr=[("LC", 0, 16)], oap=T.LC[:, 0:16])
+        tt("m1", "l2", "l3", A.max)
+        tt("m2", "l4", "H1", A.max)
+        emit("v", lambda: V.tensor_tensor(T.ZI[:, 0:16], ap(reg("m1")), ap(reg("m2")), A.max), [reg("m1"), reg("m2")], [("ZI", 0, 16)])
+        z = ("ZI", 0, 16)
+        ts("t1", z, "k", 2.0, A.min, A.mult)
+        ts("t2", z, "n2", None, A.min)
+        ts("t3", z, "n3", None, A.min)
+        ts("q1", z, "k", 2.0, A.is_ge, A.mult)
+        ts("zn", z, "n2", 0.25, A.is_ge, A.mult)
+        tt("u", "t2", "t3", A.add)
+        ts("zk", z, "k", 0.5, A.subtract, A.add)
+        tt("N", "u", "t1", A.add)
+        tt("i", "q1", "J", A.add)
+        for b in range(4):
+            mm(b, 128, "E", 128 * b, QX, AWID - 128)
+            psum_copy("v" if b == 0 else "s", T.AW[:, AWID * b + C:AWID * b + AWID], ("AW", AWID * b + C, AWID * b + AWID), b, 128 - K, 128, 1.0 / 64)
+        for b in range(4):
+            w = T.AW[:, AWID * b:AWID * b + AWID]
+            emit("v", lambda: V.tensor_tensor(T.ZT[:, b:4 * C:4], w.indirect(T.LC[:, 0:16]), T.FH[:, C * b:C * b + C], A.add),
+                 [("AW", AWID * b, AWID * b + AWID), ("FH", C * b, C * b + C), ("LC", 0, 16)], [("ZT#%d" % b, 0, C)])
+        quant("QZ", 0, C, "ZT", 0, lanes("ZT", 0, C))
+        if t == 0:
+            pre("t", [("Ws", 0, 512)], [])
+        for b in range(4):
+            mm(4 + b, C, "W", 128 * b, "QZ", 0, False, True)
+        tt("I", "i", "N", A.subtract)
+        ts("mo", "I", 2.0, 4.0, A.is_ge, A.mult)
+        tt("x1", "mo", "zn", A.mult)
+        ts("km", "mo", "k", 0.5, A.mult, A.mult)
+        tt("lf", "I", "x1", A.add)
+        tt("D", "zk", "km", A.add)
+        ts("lg", "lf", -2.0, 1.0, A.mult, A.add)
+        tt("gg", "lg", "mo", A.add)
+        tt("gD", "gg", "D", A.mult)
+        ts(None, "gD", "c", -0.5, A.add, A.add, wr=[("LO", 0, 16)], oap=T.LO[:, 0:16])
+        if t == 0:
+            quant("QV", 0, 128, "VT", 0, [("VT", 0, 512)])
+            for i in (1, 2):
+                fill("XW%d" % i, 0, XB, 0.0, lanes("XW%d" % i, -PAD, 0))
+                fill("XW%d" % i, XB + 4 * C, XWID, 0.0, lanes("XW%d" % i, C, C + PAD))
+        for b in range(4):
+            psum_copy("vs"[b % 2], T.YS[:, C * b:C * b + C], ("YS", C * b, C * b + C), 4 + b, 0, C, 0.03125)
+
+        def page(q, b, a, n):
+            gather(q, T[NX][:, XB + 4 * a + b:XB + 4 * a + 4 * n:4], T.YS[:, C * b:C * b + C], T.LO[:, a // 16:(a + n) // 16],
+                   [("YS", C * b, C * b + C), ("LO", 0, 16)], [(NX + "#%d" % b, a, a + n)])
+        for b in range(4):
+            if last:
+                page("vs"[b % 2], b, 0, C)
+            else:
+                page("vs"[b % 2], b, 64, 128)
+        if not last:
+            for b in (1, 3, 2):
+                page("s", b, 0, 64)
+                page("s", b, 192, 64)
+    XW, QX = "XW%d" % R, "QX%d" % R
+    for h in range(2):
+        quant(QX, 128 * h, 128, XW, XB + 512 * h, lanes(XW, 128 * h, 128 * h + 128))
+    for h in range(2):
+        mm(h, 128, "QV", 0, QX, 128 * h)
+        psum_copy("v", T.YO[:, 128 * h:128 * h + 128], ("YO", 128 * h, 128 * h + 128), h, 0, 128, 1.0)
+    gather("s", T.LOF[:, 0:C], T.PLACE[:, 0:C], T.LO[:, 0:16], [("PLACE", 0, C), ("LO", 0, 16)], [("LOF", 0, C)])
+    dma("y", "oc", T.oc[:, 0:4 * C], T[QX + "c"][:, 0:C].bitcast(dt.uint8), [(QX, 0, C)], [])
+    dma("s", "lo", T.lo[:, 0:C], T.LOF[0:128:16, 0:C], [("LOF", 0, C)], [])
+    for i in range(4):
+        dma("yyss"[i], "os%d" % i, T.osc[4 * i:4 * i + 4, 0:C], T[QX + "p"][32 * i:32 * i + 4, 0:C], [(QX, 0, C)], [])
+    for h in range(2):
+        dma("y", "y%d" % h, T.y[:, 128 * h:128 * h + 128], T.YO[:, 128 * h:128 * h + 128], [("YO", 128 * h, 128 * h + 128)], [])
+    for sem in sorted(count, key=lambda s: (s[0] == "d", s)):
+        if waited.get(sem, 0) < count[sem]:
+            wait("g", (sem, count[sem]))

@@ -5,18 +5,19 @@ PAD = 80
 XWID = 4 * (C + 2 * PAD)
 XB = 4 * PAD
 AWID = C + K
+BIG = 1000.0
 
 WORK = {}
 _n = [0]
 for _name, _w in (("NEG", 72), ("PC", 72), ("PK", 24), ("MC", 72), ("MK", 24), ("C4", 1), ("K4", 1), ("S15", 1), ("T3", 1),
-                  ("QT", 1), ("J", 16), ("J1", 16), ("J3", 16), ("H1", 16), ("J2A", 16), ("J2B", 16), ("I1", 16), ("ZQ", 8),
-                  ("mk", 8), ("hb", 8), ("f", 1), ("b1", 8), ("a1", 8), ("q", 8), ("r0", 8), ("r", 8),
-                  ("c", 1), ("k", 1), ("n3", 1), ("n2", 1), ("cpk", 1), ("k2", 1), ("c2", 1), ("tau", 1), ("st2", 1),
-                  ("w1", 1), ("w0", 1), ("rho", 1), ("th3", 1), ("a", 1),
-                  ("s1", 16), ("s2", 16), ("s3", 16), ("s4", 16), ("e1", 16), ("e2", 16), ("e3", 16), ("e4", 16), ("e5", 16),
-                  ("g1", 16), ("g2", 16), ("g3", 16), ("h1", 16), ("h2", 16), ("h3", 16), ("h4", 16), ("h5", 16), ("h6", 16),
+                  ("QT", 1), ("J", 16), ("J1", 16), ("H1", 16), ("I1", 16), ("ZQ", 8),
+                  ("mk", 8), ("f", 1), ("w1", 8), ("r0", 8), ("m", 8), ("r", 8),
+                  ("c", 1), ("k", 1), ("n3", 1), ("n2", 1), ("cpk", 1), ("k2", 1), ("c2", 1), ("tau", 1), ("kb", 1), ("km1", 1),
+                  ("nch", 1), ("nk", 1), ("nkw", 1), ("rho", 1), ("a", 1), ("Rr", 16), ("ae", 16), ("ay", 16), ("w", 16),
+                  ("x1", 16), ("x2", 16), ("x3", 16), ("y1", 16), ("y2", 16), ("v", 16), ("v0", 16), ("v1", 16), ("v2", 16),
+                  ("v3", 16), ("o1", 16), ("o2", 16), ("o3", 16), ("o4", 16), ("mn", 16), ("mm", 16),
                   ("l2", 16), ("l3", 16), ("l4", 16), ("m1", 16), ("m2", 16), ("t1", 16), ("t2", 16), ("t3", 16), ("u", 16),
-                  ("N", 16), ("i", 16), ("q1", 16), ("I", 16), ("mo", 16), ("zn", 16), ("x1", 16), ("lf", 16), ("lg", 16),
+                  ("N", 16), ("I", 16), ("mo", 16), ("zn", 16), ("xx", 16), ("lf", 16), ("lg", 16),
                   ("gg", 16), ("km", 16), ("zk", 16), ("D", 16), ("gD", 16)):
     WORK[_name] = (_n[0], _w)
     _n[0] += -(-_w // 8) * 8
@@ -28,13 +29,13 @@ SCRATCH = {
     "PLACE": ("sbuf", [128, C], "float32"), "LOF": ("sbuf", [128, C], "float32"), "YO": ("sbuf", [128, C], "float32"),
     "UO": ("sbuf", [128, 16], "uint16"), "LB1": ("sbuf", [128, 16], "uint16"), "LB2": ("sbuf", [128, 8], "uint16"),
     "LC": ("sbuf", [128, 16], "uint16"), "LO": ("sbuf", [128, 16], "uint16"),
-    "ONE": ("sbuf", [128, 516], "bfloat16"), "EB": ("sbuf", [128, 516], "bfloat16"),
+    "ONE": ("sbuf", [128, 516], "bfloat16"), "EB": ("sbuf", [128, 516], "bfloat16"), "EB2": ("sbuf", [128, 516], "bfloat16"),
     "UT": ("sbuf", [128, 512], "bfloat16"), "VT": ("sbuf", [128, 512], "bfloat16"), "BT": ("sbuf", [128, 512], "bfloat16"),
     "ZT": ("sbuf", [128, 4 * C], "bfloat16"), "YS": ("sbuf", [128, 4 * C], "bfloat16"), "AW": ("sbuf", [128, 4 * AWID], "bfloat16"),
-    "FH": ("sbuf", [128, 4 * C], "bfloat16"),
+    "FH": ("sbuf", [128, 2 * C], "bfloat16"), "AS": ("sbuf", [128, 2 * C], "bfloat16"),
 }
-for _name, _w in (("E", 512), ("QU", 128), ("UC", 256), ("QV", 128), ("W", 512), ("QZ", 256), ("QM0", 128), ("QM1", 128), ("QM2", 128),
-                  ("QX0", AWID), ("QX1", AWID), ("QX2", AWID), ("QX3", C), ("QB0", 128), ("QB1", 128), ("QB2", 128)):
+for _name, _w in (("E", 512), ("EH", 256), ("QU", 128), ("UC", 256), ("QV", 128), ("W", 512), ("QZ", 256), ("QM0", 128), ("QM1", 128),
+                  ("QM2", 128), ("QX0", AWID), ("QX1", AWID), ("QX2", AWID), ("QX3", C), ("QB0", 128), ("QB1", 128), ("QB2", 128)):
     SCRATCH[_name + "c"] = ("sbuf", [128, _w], "float8_e4m3fn_x4")
     SCRATCH[_name + "p"] = ("sbuf", [128, _w], "uint8")
 for _t in range(R + 1):
@@ -133,8 +134,8 @@ def rank_program(g, core, T, topo):
     def lanes(name, a, b):
         return [(name + "#%d" % i, a, b) for i in range(4)]
 
-    def ts(out, in0, s1, s2, op0, op1=None, wr=None, oap=None):
-        out, in0 = (norm(out) if out is not None else None), norm(in0)
+    def ts(out, in0, s1, s2, op0, op1=None):
+        out, in0 = norm(out), norm(in0)
         rd = [in0]
         sc = []
         for s in (s1, s2):
@@ -143,24 +144,23 @@ def rank_program(g, core, T, topo):
                 rd.append(s)
                 s = ap(s)
             sc.append(s)
-        o = ap(out) if oap is None else oap
         if op1 is None:
-            emit("v", lambda: V.tensor_scalar(o, ap(in0), sc[0], None, op0), rd, wr or [out])
+            emit("v", lambda: V.tensor_scalar(ap(out), ap(in0), sc[0], None, op0), rd, [out])
         else:
-            emit("v", lambda: V.tensor_scalar(o, ap(in0), sc[0], sc[1], op0, op1), rd, wr or [out])
+            emit("v", lambda: V.tensor_scalar(ap(out), ap(in0), sc[0], sc[1], op0, op1), rd, [out])
 
     def tt(out, x, y, op):
         out, x, y = norm(out), norm(x), norm(y)
         emit("v", lambda: V.tensor_tensor(ap(out), ap(x), ap(y), op), [x, y], [out])
 
-    def ident(out, x, scale, bias):
+    def act(out, x, scale, bias, func=F.Identity):
         out, x = norm(out), norm(x)
         rd = [x]
         if isinstance(bias, str):
             bias = norm(bias)
             rd.append(bias)
             bias = ap(bias)
-        emit("s", lambda: S.activation(ap(out), ap(x), F.Identity, bias=bias, scale=scale), rd, [out])
+        emit("s", lambda: S.activation(ap(out), ap(x), func, bias=bias, scale=scale), rd, [out])
 
     def quant(dst, a, n, src, sa, rd):
         emit("v", lambda: V.quantize_mx(T[dst + "c"][:, a:a + n], T[dst + "p"][:, a:a + n], T[src][:, sa:sa + 4 * n]), rd, [(dst, a, a + n)])
@@ -173,13 +173,13 @@ def rank_program(g, core, T, topo):
     def fill(name, a, b, val, wr=None):
         emit("v", lambda: V.memset(T[name][:, a:b], val), [], wr or [(name, a, b)])
 
-    def psum_copy(q, out, wr, bank, a, b, scale):
-        rd = [("p%d" % bank, 0, 512)]
-        src = T["p%d" % bank][:, a:b]
+    def psum_copy(q, out, oa, bank, a, b, scale):
+        rd, wr = [("p%d" % bank, 0, 512)], [(out, oa, oa + b - a)]
+        src, to = T["p%d" % bank][:, a:b], T[out][:, oa:oa + b - a]
         if q == "v":
-            emit("v", lambda: V.tensor_scalar(out, src, scale, None, A.mult), rd, [wr])
+            emit("v", lambda: V.tensor_scalar(to, src, scale, None, A.mult), rd, wr)
         else:
-            emit("s", lambda: S.activation(out, src, F.Copy, scale=scale), rd, [wr])
+            emit("s", lambda: S.activation(to, src, F.Copy, scale=scale), rd, wr)
 
     def gather(q, out, win, off, rd, wr):
         if q == "v":
@@ -200,23 +200,28 @@ def rank_program(g, core, T, topo):
     emit("g", lambda: g.iota(T.M16[:, 0:16], [[16, 16]], 0, 0), [], [("M16", 0, 16)])
     emit("g", lambda: g.affine_select(T.EB[:, 0:516], T.ONE[:, 0:516], [[-1, 516]], A.is_equal, 0.0, 4, 4), [("ONE", 0, 516)], [("EB", 0, 516)])
     emit("g", lambda: g.iota(T.PLACE[:, 0:C], [[1, C]], 0, 0, allow_small_or_imprecise_dtypes=True), [], [("PLACE", 0, C)])
+    fill("XW0", 0, XB, 0.0, lanes("XW0", -PAD, 0))
     fill("wk", WORK["NEG"][0], WORK["NEG"][0] + 72, -1.0e29)
     fill("wk", WORK["MK"][0] + 17, WORK["MK"][0] + 18, 256.0)
     fill("BT", 384, 512, 0.0, lanes("BT", 96, 128))
     emit("v", lambda: V.tensor_copy(T.UO[:, 0:16], T.UI[:, 0:16]), [("UI", 0, 16)], [("UO", 0, 16)])
     ts(("I15", 0, 1), ("IP", 0, 1), 15, None, A.bitwise_and)
     ts(("I3", 0, 1), ("IP", 0, 1), 3, None, A.bitwise_and)
-    fill("XW0", 0, XB, 0.0, lanes("XW0", -PAD, 0))
+    fill("XW0", XB + 4 * C, XWID, 0.0, lanes("XW0", C, C + PAD))
     emit("v", lambda: V.tensor_copy(ap(reg("S15")), T.I15[:, 0:1]), [("I15", 0, 1)], [reg("S15")])
     emit("v", lambda: V.tensor_copy(ap(reg("T3")), T.I3[:, 0:1]), [("I3", 0, 1)], [reg("T3")])
-    fill("XW0", XB + 4 * C, XWID, 0.0, lanes("XW0", C, C + PAD))
     ts("J", ("M16", 0, 16), "S15", None, A.add)
     ts(cut("MC", 65, 66), "T3", 382.0, None, A.add)
     ts("QT", "T3", -0.25, 0.5, A.mult, A.add)
     ts("I1", "J", "T3", 322.0, A.subtract, A.add)
     ts("ZQ", cut("J", 0, 8), "T3", 258.0, A.subtract, A.add)
+    for i in (1, 2):
+        for a in (0, XB + 4 * C):
+            j = -PAD if a == 0 else C
+            emit("s", lambda: S.activation(T["XW%d" % i][:, a:a + XB], T.XW0[:, 0:XB], F.Copy), lanes("XW0", -PAD, 0), lanes("XW%d" % i, j, j + PAD))
     quant("QU", 0, 128, "UT", 0, [("UT", 0, 512)])
     emit("s", lambda: S.activation(T.UCp[:, 0:256], T.QUp[:, 0:128].indirect(T.UO[:, 0:16]), F.Copy), [("QU", 0, 128), ("UO", 0, 16)], [("UCs", 0, 256)])
+    act(("EB2", 0, 516), ("EB", 0, 516), 1.0 / 64, 0.0)
     emit("v", lambda: V.tensor_copy(T.UCc[:, 0:256].bitcast(dt.uint32), T.QUc[:, 0:128].bitcast(dt.uint32).indirect(T.UO[:, 0:16])),
          [("QU", 0, 128), ("UO", 0, 16)], [("UC", 0, 256)])
 
@@ -224,7 +229,6 @@ def rank_program(g, core, T, topo):
     rid, pid = topo.addr(dst)[:2]
     mask = topo.mask(core, dst)
     lands = 2 * len(topo.engines(core, dst))
-    order = [2, 3, 0, 1]
 
     for t in range(R):
         last = t == R - 1
@@ -247,16 +251,14 @@ def rank_program(g, core, T, topo):
         ts(cut("MC", 0, 65), cut("PC", 0, 65), cut("PC", 64, 65), 4.0, A.is_lt, A.mult)
         emit("v", lambda: V.tensor_reduce(ap(reg("K4")), ap(cut("MK", 0, 18)), AxisListType.X, A.add), [cut("MK", 0, 18)], [reg("K4")])
         emit("v", lambda: V.tensor_reduce(ap(reg("C4")), ap(cut("MC", 0, 66)), AxisListType.X, A.add), [cut("MC", 0, 66)], [reg("C4")])
-        ts("mk", "ZQ", "K4", None, A.is_gt)
-        ts(None, "I1", "C4", "K4", A.add, A.subtract, wr=[("LB1", 0, 16)], oap=T.LB1[:, 0:16])
-        ts("hb", "ZQ", "K4", None, A.add)
+        ts("mk", "ZQ", "K4", -2.0, A.is_gt, A.mult)
+        ts(("LB1", 0, 16), "I1", "C4", "K4", A.add, A.subtract)
         ts("f", "K4", 2.0, "C4", A.mult, A.is_lt)
-        tt("b1", "hb", "mk", A.mult)
-        ts("a1", "ZQ", "K4", 0.0, A.subtract, A.min)
-        ts("q", "b1", "f", -2.0, A.mult, A.mult)
-        tt("r0", "a1", "b1", A.add)
-        tt("r", "r0", "q", A.add)
-        ts(None, "r", "C4", float(XB), A.add, A.add, wr=[("LB2", 0, 8)], oap=T.LB2[:, 0:8])
+        ts("w1", "mk", "K4", "K4", A.mult, A.add)
+        ts("m", "mk", "f", 1.0, A.mult, A.add)
+        tt("r0", "ZQ", "w1", A.subtract)
+        tt("r", "r0", "m", A.mult)
+        ts(("LB2", 0, 8), "r", "C4", float(XB), A.add, A.add)
         allx = lanes(XW, -PAD, C + PAD)
         gather("s", T.BT[:, 0:256], T[XW][:, 0:XWID], T.LB1[:, 0:16], allx + [("LB1", 0, 16)], lanes("BT", 0, 64))
         gather("v", T.BT[:, 256:384], T[XW][:, 0:XWID], T.LB2[:, 0:8], allx + [("LB2", 0, 8)], lanes("BT", 64, 96))
@@ -269,101 +271,111 @@ def rank_program(g, core, T, topo):
         count["arr%d" % t] = lands
         count["loc%d" % t] = lands
         note("remote", QX, C, AWID, True, ("arr%d" % t, lands))
+        act("c", "C4", 0.25, "QT")
+        act("k2", "K4", 0.5, 0.0)
+        act("cpk", "K4", 0.25, "c")
+        act("n3", "K4", -0.25, "c")
+        act("c2", "c", 2.0, -256.5)
+        act("nch", "c", -1.0, 0.5)
+        act("n2", "cpk", -1.0, 256.0)
+        act("Rr", "J", -1.0, "c2")
+        act("nk", "K4", -0.25, 0.0)
+        act("ae", "J", 1.0, "nch", F.Abs)
+        act("nkw", "K4", -0.5, -255.5)
+        act("tau", "cpk", 2.0, -256.0)
+        act("ay", "ae", 1.0, "nk", F.Abs)
+        act("w", "J", 1.0, "nkw")
+        act("k", "K4", 0.25, 0.0)
+        act("kb", "K4", 0.25, -128.25)
+        act("km1", "K4", 0.25, -1.0)
+        act("l3", "J", 0.5, "kb")
         quant(QX, 0, C, XW, XB, lanes(XW, 0, C))
         if t == 0:
             for b in range(4):
                 quant("E", 128 * b, 128, "EB", 4 - b, [("EB", 0, 516)])
         for b in range(4):
             mm(b, C, "E", 128 * b, QX, 0)
-        for b in order:
+        for b in (2, 3, 0, 1):
             mm(4 + b, C, "E", 128 * b, QX, 0, True, False)
-        ident("c", "C4", 0.25, "QT")
-        ident("k", "K4", 0.25, 0.0)
-        ident("k2", "K4", 0.5, 0.0)
-        ident("cpk", "K4", 0.25, "c")
-        ident("n3", "K4", -0.25, "c")
-        ident("c2", "c", 2.0, 0.0)
-        ident("n2", "cpk", -1.0, 256.0)
-        ident("tau", "cpk", 2.0, -256.0)
-        ident("w1", "k2", 1.0, "cpk")
-        ident("w0", "c2", 1.0, "cpk")
-        ident("st2", "k2", 1.0, "n2")
-        for b in range(4):
-            psum_copy("s", T.AW[:, AWID * b:AWID * b + C], ("AW", AWID * b, AWID * b + C), b, 0, C, 1.0 / 64)
-            psum_copy("s", T.FH[:, C * b:C * b + C], ("FH", C * b, C * b + C), b, 0, C, 1.0 / 64)
+        for b in (0, 1):
+            psum_copy("s", "AW", AWID * b, b, 0, C, 1.0 / 64)
+        for b in (0, 1):
+            psum_copy("s", "FH", C * b, b, 0, C, 1.0 / 64)
+        for b in (2, 3):
+            psum_copy("s", "AW", AWID * b, b, 0, C, 1.0 / 64)
         if t == 0:
+            for b in (2, 3):
+                quant("EH", 128 * b - 256, 128, "EB2", 4 - b, [("EB2", 0, 516)])
             ts("J1", "J", -1.0, None, A.add)
-            ts("J3", "J", -256.5, None, A.add)
             ts("H1", "J", 0.25, -0.375, A.mult, A.add)
-            ts("J2A", "J", 2.0, -255.0, A.mult, A.add)
-            ts("J2B", "J", 2.0, 257.0, A.mult, A.add)
+            quant("QV", 0, 128, "VT", 0, [("VT", 0, 512)])
+        ts("x1", "J", "n3", BIG, A.is_lt, A.mult)
+        ts("x2", "J", "c", "k2", A.is_ge, A.mult)
+        ts("x3", "J", "cpk", "k2", A.is_ge, A.mult)
         ts("rho", "k2", "c", None, A.max)
-        ts("th3", "tau", "c", None, A.max)
-        ts("s1", "J", "n3", "n2", A.is_ge, A.mult)
-        ts("s2", "J", "c", "st2", A.is_ge, A.mult)
-        ts("s3", "J", "th3", "n2", A.is_ge, A.mult)
-        ts("s4", "J", "cpk", "k2", A.is_ge, A.mult)
-        ts("e1", "J", "tau", None, A.is_lt)
-        ts("e2", "J2A", "w1", None, A.subtract)
-        ts("e3", "J", "rho", None, A.is_ge)
-        ts("g1", "J", "c2", None, A.is_ge)
-        ts("g2", "J2B", "w0", None, A.subtract)
-        tt("h1", "s2", "s1", A.subtract)
-        tt("h2", "s3", "s4", A.add)
-        tt("e4", "e1", "e2", A.mult)
-        tt("g3", "g1", "g2", A.mult)
-        tt("h3", "h1", "h2", A.subtract)
-        tt("e5", "e4", "e3", A.mult)
-        tt("h4", "g3", "J", A.subtract)
+        tt("y1", "Rr", "x1", A.add)
+        tt("y2", "x2", "x3", A.subtract)
+        ts("o1", "J", "rho", BIG, A.is_lt, A.mult)
+        ts("o2", "J", "tau", BIG, A.is_ge, A.mult)
+        tt("v", "y1", "y2", A.add)
+        tt("o3", "o1", "o2", A.add)
         ts("a", "n2", "n3", None, A.min)
-        tt("h5", "e5", "h3", A.add)
-        ts("l3", "J3", "k2", 0.5, A.add, A.mult)
+        ts("v0", "v", -0.5, BIG, A.is_gt, A.mult)
+        ts("v1", "v", -255.75, BIG, A.is_lt, A.mult)
+        tt("o4", "o3", "w", A.add)
         ts("l2", "J1", "a", 1.0 / 3, A.subtract, A.mult)
-        tt("h6", "h5", "h4", A.add)
+        tt("v2", "v0", "v1", A.add)
+        tt("mn", "o4", "ay", A.min)
+        tt("v3", "v2", "v", A.add)
         ts("l4", "J", "k2", "a", A.subtract, A.subtract)
-        ts(None, "h6", "n3", 255.0, A.add, A.add, wr=[("LC", 0, 16)], oap=T.LC[:, 0:16])
         tt("m1", "l2", "l3", A.max)
+        tt("mm", "v3", "mn", A.min)
         tt("m2", "l4", "H1", A.max)
-        emit("v", lambda: V.tensor_tensor(T.ZI[:, 0:16], ap(reg("m1")), ap(reg("m2")), A.max), [reg("m1"), reg("m2")], [("ZI", 0, 16)])
+        ts(("LC", 0, 16), "mm", 255.5, None, A.add)
+        tt(("ZI", 0, 16), "m1", "m2", A.max)
         z = ("ZI", 0, 16)
-        ts("t1", z, "k", 2.0, A.min, A.mult)
         ts("t2", z, "n2", None, A.min)
         ts("t3", z, "n3", None, A.min)
-        ts("q1", z, "k", 2.0, A.is_ge, A.mult)
-        ts("zn", z, "n2", 0.25, A.is_ge, A.mult)
+        ts("t1", z, "km1", 2.0, A.min, A.mult)
         tt("u", "t2", "t3", A.add)
-        ts("zk", z, "k", 0.5, A.subtract, A.add)
+        ts("zn", z, "n2", 0.25, A.is_ge, A.mult)
         tt("N", "u", "t1", A.add)
-        tt("i", "q1", "J", A.add)
-        for b in range(4):
-            mm(b, 128, "E", 128 * b, QX, AWID - 128)
-            psum_copy("v" if b == 0 else "s", T.AW[:, AWID * b + C:AWID * b + AWID], ("AW", AWID * b + C, AWID * b + AWID), b, 128 - K, 128, 1.0 / 64)
-        for b in range(4):
+        ts("zk", z, "k", 0.5, A.subtract, A.add)
+        tt("I", "J", "N", A.subtract)
+        ts("mo", "I", 2.0, 4.0, A.is_ge, A.mult)
+        tt("xx", "mo", "zn", A.mult)
+        ts("km", "mo", "k", 0.5, A.mult, A.mult)
+        tt("lf", "I", "xx", A.add)
+        tt("D", "zk", "km", A.add)
+        mm(0, 128, "E", 0, QX, AWID - 128)
+        mm(2, AWID, "EH", 0, QX, 0)
+        mm(1, 128, "E", 128, QX, AWID - 128)
+        mm(3, AWID, "EH", 128, QX, 0)
+        psum_copy("v", "AW", C, 0, 128 - K, 128, 1.0 / 64)
+        psum_copy("s", "AW", AWID * 2 + C, 2, C, AWID, 1.0)
+        psum_copy("s", "AW", AWID + C, 1, 128 - K, 128, 1.0 / 64)
+        psum_copy("s", "AW", AWID * 3 + C, 3, C, AWID, 1.0)
+        for b in (2, 3):
+            gather("s", T.AS[:, C * b - 2 * C:C * b - C], T.AW[:, AWID * b:AWID * b + AWID], T.LC[:, 0:16],
+                   [("AW", AWID * b, AWID * b + AWID), ("LC", 0, 16)], [("AS", C * b - 2 * C, C * b - C)])
+        for b in (0, 1):
             w = T.AW[:, AWID * b:AWID * b + AWID]
             emit("v", lambda: V.tensor_tensor(T.ZT[:, b:4 * C:4], w.indirect(T.LC[:, 0:16]), T.FH[:, C * b:C * b + C], A.add),
                  [("AW", AWID * b, AWID * b + AWID), ("FH", C * b, C * b + C), ("LC", 0, 16)], [("ZT#%d" % b, 0, C)])
+        for b in (2, 3):
+            emit("v", lambda: V.tensor_tensor(T.ZT[:, b:4 * C:4], T.AS[:, C * b - 2 * C:C * b - C], T["p%d" % b][:, 0:C], A.add),
+                 [("AS", C * b - 2 * C, C * b - C), ("p%d" % b, 0, 512)], [("ZT#%d" % b, 0, C)])
         quant("QZ", 0, C, "ZT", 0, lanes("ZT", 0, C))
         if t == 0:
             pre("t", [("Ws", 0, 512)], [])
         for b in range(4):
             mm(4 + b, C, "W", 128 * b, "QZ", 0, False, True)
-        tt("I", "i", "N", A.subtract)
-        ts("mo", "I", 2.0, 4.0, A.is_ge, A.mult)
-        tt("x1", "mo", "zn", A.mult)
-        ts("km", "mo", "k", 0.5, A.mult, A.mult)
-        tt("lf", "I", "x1", A.add)
-        tt("D", "zk", "km", A.add)
         ts("lg", "lf", -2.0, 1.0, A.mult, A.add)
         tt("gg", "lg", "mo", A.add)
         tt("gD", "gg", "D", A.mult)
-        ts(None, "gD", "c", -0.5, A.add, A.add, wr=[("LO", 0, 16)], oap=T.LO[:, 0:16])
-        if t == 0:
-            quant("QV", 0, 128, "VT", 0, [("VT", 0, 512)])
-            for i in (1, 2):
-                fill("XW%d" % i, 0, XB, 0.0, lanes("XW%d" % i, -PAD, 0))
-                fill("XW%d" % i, XB + 4 * C, XWID, 0.0, lanes("XW%d" % i, C, C + PAD))
+        ts(("LO", 0, 16), "gD", "c", -0.5, A.add, A.add)
         for b in range(4):
-            psum_copy("vs"[b % 2], T.YS[:, C * b:C * b + C], ("YS", C * b, C * b + C), 4 + b, 0, C, 0.03125)
+            psum_copy("vs"[b % 2], "YS", C * b, 4 + b, 0, C, 0.03125)
 
         def page(q, b, a, n):
             gather(q, T[NX][:, XB + 4 * a + b:XB + 4 * a + 4 * n:4], T.YS[:, C * b:C * b + C], T.LO[:, a // 16:(a + n) // 16],
@@ -382,7 +394,7 @@ def rank_program(g, core, T, topo):
         quant(QX, 128 * h, 128, XW, XB + 512 * h, lanes(XW, 128 * h, 128 * h + 128))
     for h in range(2):
         mm(h, 128, "QV", 0, QX, 128 * h)
-        psum_copy("v", T.YO[:, 128 * h:128 * h + 128], ("YO", 128 * h, 128 * h + 128), h, 0, 128, 1.0)
+        psum_copy("v", "YO", 128 * h, h, 0, 128, 1.0)
     gather("s", T.LOF[:, 0:C], T.PLACE[:, 0:C], T.LO[:, 0:16], [("PLACE", 0, C), ("LO", 0, 16)], [("LOF", 0, C)])
     dma("y", "oc", T.oc[:, 0:4 * C], T[QX + "c"][:, 0:C].bitcast(dt.uint8), [(QX, 0, C)], [])
     dma("s", "lo", T.lo[:, 0:C], T.LOF[0:128:16, 0:C], [("LOF", 0, C)], [])

@@ -13,11 +13,12 @@ for _name, _w in (("NEG", 72), ("PC", 72), ("PK", 24), ("MC", 72), ("MK", 24), (
                   ("QT", 1), ("J", 16), ("J1", 16), ("H1", 16), ("I1", 16), ("ZQ", 8),
                   ("mk", 8), ("f", 1), ("w1", 8), ("r0", 8), ("m", 8), ("r", 8),
                   ("c", 1), ("k", 1), ("n3", 1), ("n2", 1), ("cpk", 1), ("k2", 1), ("c2", 1), ("tau", 1), ("kb", 1), ("km1", 1),
-                  ("nch", 1), ("nk", 1), ("nkw", 1), ("rho", 1), ("a", 1), ("Rr", 16), ("ae", 16), ("ay", 16), ("w", 16),
+                  ("nch", 1), ("nk", 1), ("nkw", 1), ("rl", 1), ("rho", 1), ("br", 1), ("bt", 1), ("bn", 1), ("a", 1),
+                  ("Rr", 16), ("ae", 16), ("ay", 16), ("w", 16),
                   ("x1", 16), ("x2", 16), ("x3", 16), ("y1", 16), ("y2", 16), ("v", 16), ("v0", 16), ("v1", 16), ("v2", 16),
                   ("v3", 16), ("o1", 16), ("o2", 16), ("o3", 16), ("o4", 16), ("mn", 16), ("mm", 16),
                   ("l2", 16), ("l3", 16), ("l4", 16), ("m1", 16), ("m2", 16), ("t1", 16), ("t2", 16), ("t3", 16), ("u", 16),
-                  ("N", 16), ("I", 16), ("mo", 16), ("zn", 16), ("xx", 16), ("lf", 16), ("lg", 16),
+                  ("N", 16), ("I", 16), ("mo", 16), ("zl", 16), ("xx", 16), ("ti", 16),
                   ("gg", 16), ("km", 16), ("zk", 16), ("D", 16), ("gD", 16)):
     WORK[_name] = (_n[0], _w)
     _n[0] += -(-_w // 8) * 8
@@ -156,7 +157,7 @@ def rank_program(g, core, T, topo):
     def act(out, x, scale, bias, func=F.Identity):
         out, x = norm(out), norm(x)
         rd = [x]
-        if isinstance(bias, str):
+        if isinstance(bias, (str, tuple)):
             bias = norm(bias)
             rd.append(bias)
             bias = ap(bias)
@@ -207,7 +208,6 @@ def rank_program(g, core, T, topo):
     emit("v", lambda: V.tensor_copy(T.UO[:, 0:16], T.UI[:, 0:16]), [("UI", 0, 16)], [("UO", 0, 16)])
     ts(("I15", 0, 1), ("IP", 0, 1), 15, None, A.bitwise_and)
     ts(("I3", 0, 1), ("IP", 0, 1), 3, None, A.bitwise_and)
-    fill("XW0", XB + 4 * C, XWID, 0.0, lanes("XW0", C, C + PAD))
     emit("v", lambda: V.tensor_copy(ap(reg("S15")), T.I15[:, 0:1]), [("I15", 0, 1)], [reg("S15")])
     emit("v", lambda: V.tensor_copy(ap(reg("T3")), T.I3[:, 0:1]), [("I3", 0, 1)], [reg("T3")])
     ts("J", ("M16", 0, 16), "S15", None, A.add)
@@ -215,11 +215,13 @@ def rank_program(g, core, T, topo):
     ts("QT", "T3", -0.25, 0.5, A.mult, A.add)
     ts("I1", "J", "T3", 322.0, A.subtract, A.add)
     ts("ZQ", cut("J", 0, 8), "T3", 258.0, A.subtract, A.add)
+    fill("XW0", XB + 4 * C, XWID, 0.0, lanes("XW0", C, C + PAD))
     for i in (1, 2):
         for a in (0, XB + 4 * C):
             j = -PAD if a == 0 else C
             emit("s", lambda: S.activation(T["XW%d" % i][:, a:a + XB], T.XW0[:, 0:XB], F.Copy), lanes("XW0", -PAD, 0), lanes("XW%d" % i, j, j + PAD))
     quant("QU", 0, 128, "UT", 0, [("UT", 0, 512)])
+    quant("QM0", 0, 128, "XW0", XB + 4 * 64, lanes("XW0", 64, 192))
     emit("s", lambda: S.activation(T.UCp[:, 0:256], T.QUp[:, 0:128].indirect(T.UO[:, 0:16]), F.Copy), [("QU", 0, 128), ("UO", 0, 16)], [("UCs", 0, 256)])
     act(("EB2", 0, 516), ("EB", 0, 516), 1.0 / 64, 0.0)
     emit("v", lambda: V.tensor_copy(T.UCc[:, 0:256].bitcast(dt.uint32), T.QUc[:, 0:128].bitcast(dt.uint32).indirect(T.UO[:, 0:16])),
@@ -230,19 +232,23 @@ def rank_program(g, core, T, topo):
     mask = topo.mask(core, dst)
     lands = 2 * len(topo.engines(core, dst))
 
+    def e_tile(b):
+        return ("E", 128 * b, 1.0 / 64) if b < 2 else ("EH", 128 * b - 256, 1.0)
+
     for t in range(R):
         last = t == R - 1
         XW, QX, QM, QB = "XW%d" % t, "QX%d" % t, "QM%d" % t, "QB%d" % t
         NX = "XW%d" % (t + 1)
-        quant(QM, 0, 128, XW, XB + 4 * 64, lanes(XW, 64, 192))
         if t == 0:
             pre("t", [("UCs", 0, 256)], [])
+        else:
+            quant(QM, 0, 128, XW, XB + 4 * 64, lanes(XW, 64, 192))
         mm(5, 128, "UC", 128, QM, 0)
         mm(4, 128, "UC", 0, QM, 0)
         if t > 0:
             for a in (0, 192):
-                gather("v", T[XW][:, XB + 4 * a:XB + 4 * a + 256:4], T.YS[:, 0:C], T.LO[:, a // 16:a // 16 + 4],
-                       [("YS", 0, C), ("LO", 0, 16)], [(XW + "#0", a, a + 64)])
+                gather("v", T[XW][:, XB + 4 * a + 1:XB + 4 * a + 256:4], T.YS[:, C:2 * C], T.LO[:, a // 16:a // 16 + 4],
+                       [("YS", C, 2 * C), ("LO", 0, 16)], [(XW + "#1", a, a + 64)])
         emit("v", lambda: V.tensor_tensor_scan(ap(cut("PK", 0, 17)), T.p5[:, 0:17], ap(cut("NEG", 0, 17)), -1.0e29, A.max, A.max),
              [("p5", 0, 512), reg("NEG")], [cut("PK", 0, 17)])
         emit("v", lambda: V.tensor_tensor_scan(ap(cut("PC", 0, 65)), T.p4[:, 32:97], ap(cut("NEG", 0, 65)), -1.0e29, A.max, A.max),
@@ -251,14 +257,20 @@ def rank_program(g, core, T, topo):
         ts(cut("MC", 0, 65), cut("PC", 0, 65), cut("PC", 64, 65), 4.0, A.is_lt, A.mult)
         emit("v", lambda: V.tensor_reduce(ap(reg("K4")), ap(cut("MK", 0, 18)), AxisListType.X, A.add), [cut("MK", 0, 18)], [reg("K4")])
         emit("v", lambda: V.tensor_reduce(ap(reg("C4")), ap(cut("MC", 0, 66)), AxisListType.X, A.add), [cut("MC", 0, 66)], [reg("C4")])
+        act("k2", "K4", 0.5, 0.0)
+        act("c", "C4", 0.25, "QT")
         ts("mk", "ZQ", "K4", -2.0, A.is_gt, A.mult)
         ts(("LB1", 0, 16), "I1", "C4", "K4", A.add, A.subtract)
         ts("f", "K4", 2.0, "C4", A.mult, A.is_lt)
         ts("w1", "mk", "K4", "K4", A.mult, A.add)
+        act("cpk", "K4", 0.25, "c")
         ts("m", "mk", "f", 1.0, A.mult, A.add)
         tt("r0", "ZQ", "w1", A.subtract)
+        ts("x2", "J", "c", "k2", A.is_ge, A.mult)
         tt("r", "r0", "m", A.mult)
+        ts("x3", "J", "cpk", "k2", A.is_ge, A.mult)
         ts(("LB2", 0, 8), "r", "C4", float(XB), A.add, A.add)
+        tt("y2", "x2", "x3", A.subtract)
         allx = lanes(XW, -PAD, C + PAD)
         gather("s", T.BT[:, 0:256], T[XW][:, 0:XWID], T.LB1[:, 0:16], allx + [("LB1", 0, 16)], lanes("BT", 0, 64))
         gather("v", T.BT[:, 256:384], T[XW][:, 0:XWID], T.LB2[:, 0:8], allx + [("LB2", 0, 8)], lanes("BT", 64, 96))
@@ -271,93 +283,89 @@ def rank_program(g, core, T, topo):
         count["arr%d" % t] = lands
         count["loc%d" % t] = lands
         note("remote", QX, C, AWID, True, ("arr%d" % t, lands))
-        act("c", "C4", 0.25, "QT")
-        act("k2", "K4", 0.5, 0.0)
-        act("cpk", "K4", 0.25, "c")
         act("n3", "K4", -0.25, "c")
         act("c2", "c", 2.0, -256.5)
-        act("nch", "c", -1.0, 0.5)
+        act("rl", "k2", -1.0, "c", F.Relu)
         act("n2", "cpk", -1.0, 256.0)
-        act("Rr", "J", -1.0, "c2")
-        act("nk", "K4", -0.25, 0.0)
-        act("ae", "J", 1.0, "nch", F.Abs)
-        act("nkw", "K4", -0.5, -255.5)
-        act("tau", "cpk", 2.0, -256.0)
-        act("ay", "ae", 1.0, "nk", F.Abs)
-        act("w", "J", 1.0, "nkw")
-        act("k", "K4", 0.25, 0.0)
+        act("bn", "n3", BIG, 0.0)
         act("kb", "K4", 0.25, -128.25)
-        act("km1", "K4", 0.25, -1.0)
+        act("Rr", "J", -1.0, "c2")
+        act("x1", "J", -BIG, "bn", F.Relu)
         act("l3", "J", 0.5, "kb")
+        act("tau", "cpk", 2.0, -256.0)
+        act("rho", "rl", 1.0, "k2")
+        act("nkw", "K4", -0.5, -255.5)
+        act("bt", "tau", -BIG, BIG)
+        act("br", "rho", BIG, 0.0)
+        act("nch", "c", -1.0, 0.5)
+        act("o2", "J", BIG, "bt", F.Relu)
+        act("o1", "J", -BIG, "br", F.Relu)
+        act("w", "J", 1.0, "nkw")
+        act("ae", "J", 1.0, "nch", F.Abs)
+        act("nk", "K4", -0.25, 0.0)
+        act("k", "K4", 0.25, 0.0)
+        act("ay", "ae", 1.0, "nk", F.Abs)
+        act("km1", "K4", 0.25, -1.0)
         quant(QX, 0, C, XW, XB, lanes(XW, 0, C))
         if t == 0:
-            for b in range(4):
+            for b in (0, 1):
                 quant("E", 128 * b, 128, "EB", 4 - b, [("EB", 0, 516)])
-        for b in range(4):
-            mm(b, C, "E", 128 * b, QX, 0)
-        for b in (2, 3, 0, 1):
-            mm(4 + b, C, "E", 128 * b, QX, 0, True, False)
-        for b in (0, 1):
-            psum_copy("s", "AW", AWID * b, b, 0, C, 1.0 / 64)
-        for b in (0, 1):
-            psum_copy("s", "FH", C * b, b, 0, C, 1.0 / 64)
-        for b in (2, 3):
-            psum_copy("s", "AW", AWID * b, b, 0, C, 1.0 / 64)
-        if t == 0:
             for b in (2, 3):
                 quant("EH", 128 * b - 256, 128, "EB2", 4 - b, [("EB2", 0, 516)])
+        for b in range(4):
+            e, ea, sc = e_tile(b)
+            mm(b, C, e, ea, QX, 0)
+            psum_copy("s", "AW", AWID * b, b, 0, C, sc)
+            if b < 2:
+                emit("g", lambda: g.affine_select(T.FH[:, C * b:C * b + C], T.AW[:, AWID * b:AWID * b + C], [[1, C]], A.is_ge, 0.0, 0, 0),
+                     [("AW", AWID * b, AWID * b + C)], [("FH", C * b, C * b + C)])
+        if t == 0:
             ts("J1", "J", -1.0, None, A.add)
             ts("H1", "J", 0.25, -0.375, A.mult, A.add)
-            quant("QV", 0, 128, "VT", 0, [("VT", 0, 512)])
-        ts("x1", "J", "n3", BIG, A.is_lt, A.mult)
-        ts("x2", "J", "c", "k2", A.is_ge, A.mult)
-        ts("x3", "J", "cpk", "k2", A.is_ge, A.mult)
-        ts("rho", "k2", "c", None, A.max)
-        tt("y1", "Rr", "x1", A.add)
-        tt("y2", "x2", "x3", A.subtract)
-        ts("o1", "J", "rho", BIG, A.is_lt, A.mult)
-        ts("o2", "J", "tau", BIG, A.is_ge, A.mult)
-        tt("v", "y1", "y2", A.add)
-        tt("o3", "o1", "o2", A.add)
         ts("a", "n2", "n3", None, A.min)
+        tt("y1", "Rr", "x1", A.add)
+        ts("l2", "J1", "a", 1.0 / 3, A.subtract, A.mult)
+        ts("l4", "J", "k2", "a", A.subtract, A.subtract)
+        tt("v", "y1", "y2", A.add)
+        tt("m1", "l2", "l3", A.max)
+        tt("m2", "l4", "H1", A.max)
         ts("v0", "v", -0.5, BIG, A.is_gt, A.mult)
         ts("v1", "v", -255.75, BIG, A.is_lt, A.mult)
-        tt("o4", "o3", "w", A.add)
-        ts("l2", "J1", "a", 1.0 / 3, A.subtract, A.mult)
-        tt("v2", "v0", "v1", A.add)
-        tt("mn", "o4", "ay", A.min)
-        tt("v3", "v2", "v", A.add)
-        ts("l4", "J", "k2", "a", A.subtract, A.subtract)
-        tt("m1", "l2", "l3", A.max)
-        tt("mm", "v3", "mn", A.min)
-        tt("m2", "l4", "H1", A.max)
-        ts(("LC", 0, 16), "mm", 255.5, None, A.add)
         tt(("ZI", 0, 16), "m1", "m2", A.max)
         z = ("ZI", 0, 16)
+        tt("v2", "v0", "v1", A.add)
+        tt("o3", "o1", "o2", A.add)
         ts("t2", z, "n2", None, A.min)
+        tt("v3", "v2", "v", A.add)
+        tt("o4", "o3", "w", A.add)
         ts("t3", z, "n3", None, A.min)
+        tt("mn", "o4", "ay", A.min)
         ts("t1", z, "km1", 2.0, A.min, A.mult)
+        tt("mm", "v3", "mn", A.min)
         tt("u", "t2", "t3", A.add)
-        ts("zn", z, "n2", 0.25, A.is_ge, A.mult)
+        ts(("LC", 0, 16), "mm", 255.5, None, A.add)
         tt("N", "u", "t1", A.add)
         ts("zk", z, "k", 0.5, A.subtract, A.add)
         tt("I", "J", "N", A.subtract)
-        ts("mo", "I", 2.0, 4.0, A.is_ge, A.mult)
-        tt("xx", "mo", "zn", A.mult)
-        ts("km", "mo", "k", 0.5, A.mult, A.mult)
-        tt("lf", "I", "xx", A.add)
-        tt("D", "zk", "km", A.add)
-        mm(0, 128, "E", 0, QX, AWID - 128)
-        mm(2, AWID, "EH", 0, QX, 0)
-        mm(1, 128, "E", 128, QX, AWID - 128)
-        mm(3, AWID, "EH", 128, QX, 0)
-        psum_copy("v", "AW", C, 0, 128 - K, 128, 1.0 / 64)
-        psum_copy("s", "AW", AWID * 2 + C, 2, C, AWID, 1.0)
-        psum_copy("s", "AW", AWID + C, 1, 128 - K, 128, 1.0 / 64)
-        psum_copy("s", "AW", AWID * 3 + C, 3, C, AWID, 1.0)
+        ts("zl", z, "n2", 1.0, A.is_lt, A.add)
+        ts("mo", "I", 2.0, 2.0, A.is_ge, A.mult)
+        ts("ti", "I", -2.0, 1.0, A.mult, A.add)
+        tt("xx", "mo", "zl", A.mult)
+        ts("km", "mo", "k", None, A.mult)
+        tt("gg", "ti", "xx", A.add)
+        if t == 0:
+            for b in (2, 3):
+                quant("E", 128 * b, 128, "EB", 4 - b, [("EB", 0, 516)])
+        for b in (0, 2, 1, 3):
+            e, ea, sc = e_tile(b)
+            mm(4 + b, 128, e, ea, QX, AWID - 128)
+        for b in (2, 3):
+            psum_copy("s", "AW", AWID * b + C, 4 + b, 128 - K, 128, 1.0)
         for b in (2, 3):
             gather("s", T.AS[:, C * b - 2 * C:C * b - C], T.AW[:, AWID * b:AWID * b + AWID], T.LC[:, 0:16],
                    [("AW", AWID * b, AWID * b + AWID), ("LC", 0, 16)], [("AS", C * b - 2 * C, C * b - C)])
+        for b in (0, 1):
+            psum_copy("v", "AW", AWID * b + C, 4 + b, 128 - K, 128, 1.0 / 64)
         for b in (0, 1):
             w = T.AW[:, AWID * b:AWID * b + AWID]
             emit("v", lambda: V.tensor_tensor(T.ZT[:, b:4 * C:4], w.indirect(T.LC[:, 0:16]), T.FH[:, C * b:C * b + C], A.add),
@@ -365,31 +373,30 @@ def rank_program(g, core, T, topo):
         for b in (2, 3):
             emit("v", lambda: V.tensor_tensor(T.ZT[:, b:4 * C:4], T.AS[:, C * b - 2 * C:C * b - C], T["p%d" % b][:, 0:C], A.add),
                  [("AS", C * b - 2 * C, C * b - C), ("p%d" % b, 0, 512)], [("ZT#%d" % b, 0, C)])
+        tt("D", "zk", "km", A.add)
         quant("QZ", 0, C, "ZT", 0, lanes("ZT", 0, C))
+        for b in (0, 2, 1, 3):
+            mm(4 + b, C, "E", 128 * b, QX, 0, True, False)
         if t == 0:
             pre("t", [("Ws", 0, 512)], [])
         for b in range(4):
             mm(4 + b, C, "W", 128 * b, "QZ", 0, False, True)
-        ts("lg", "lf", -2.0, 1.0, A.mult, A.add)
-        tt("gg", "lg", "mo", A.add)
         tt("gD", "gg", "D", A.mult)
         ts(("LO", 0, 16), "gD", "c", -0.5, A.add, A.add)
-        for b in range(4):
-            psum_copy("vs"[b % 2], "YS", C * b, 4 + b, 0, C, 0.03125)
 
         def page(q, b, a, n):
             gather(q, T[NX][:, XB + 4 * a + b:XB + 4 * a + 4 * n:4], T.YS[:, C * b:C * b + C], T.LO[:, a // 16:(a + n) // 16],
                    [("YS", C * b, C * b + C), ("LO", 0, 16)], [(NX + "#%d" % b, a, a + n)])
         for b in range(4):
-            if last:
-                page("vs"[b % 2], b, 0, C)
-            else:
-                page("vs"[b % 2], b, 64, 128)
+            psum_copy("sv"[b % 2], "YS", C * b, 4 + b, 0, C, 0.03125)
+        for b in range(4):
+            page("sv"[b % 2], b, 0 if last else 64, C if last else 128)
         if not last:
-            for b in (1, 3, 2):
+            for b in (0, 2, 3):
                 page("s", b, 0, 64)
                 page("s", b, 192, 64)
     XW, QX = "XW%d" % R, "QX%d" % R
+    quant("QV", 0, 128, "VT", 0, [("VT", 0, 512)])
     for h in range(2):
         quant(QX, 128 * h, 128, XW, XB + 512 * h, lanes(XW, 128 * h, 128 * h + 128))
     for h in range(2):

from concourse.mybir import dt, AluOpType as A, AxisListType, ActivationFunctionType as F

R, C, K = 3, 256, 96
PAD = 80
XWID = 4 * (C + 2 * PAD)
XB = 4 * PAD
AWID = C + K
BIG = 1000.0

WORK = {}
_n = [0]
for _name, _w in (("NEG", 72), ("PC", 72), ("PK", 24), ("MC", 72), ("MK", 24), ("C4", 1), ("K4", 1), ("S15", 1), ("T3", 1),
                  ("QT", 1), ("J", 16), ("J1", 16), ("H1", 16), ("I1", 16), ("ZQ", 8),
                  ("mk", 8), ("f", 1), ("w1", 8), ("r0", 8), ("m", 8), ("r", 8),
                  ("c", 1), ("k", 1), ("n3", 1), ("n2", 1), ("cpk", 1), ("k2", 1), ("c2", 1), ("tau", 1), ("kb", 1), ("km1", 1),
                  ("nch", 1), ("nk", 1), ("nkw", 1), ("rl", 1), ("rho", 1), ("br", 1), ("bt", 1), ("bn", 1), ("a", 1),
                  ("Rr", 16), ("ae", 16), ("ay", 16), ("w", 16),
                  ("x1", 16), ("x2", 16), ("x3", 16), ("y1", 16), ("y2", 16), ("v", 16), ("v0", 16), ("v1", 16), ("v2", 16),
                  ("v3", 16), ("o1", 16), ("o2", 16), ("o3", 16), ("o4", 16), ("mn", 16), ("mm", 16),
                  ("l2", 16), ("l3", 16), ("l4", 16), ("m1", 16), ("m2", 16), ("t1", 16), ("t2", 16), ("t3", 16), ("u", 16),
                  ("N", 16), ("I", 16), ("mo", 16), ("zl", 16), ("xx", 16), ("ti", 16),
                  ("gg", 16), ("km", 16), ("zk", 16), ("D", 16), ("gD", 16)):
    WORK[_name] = (_n[0], _w)
    _n[0] += -(-_w // 8) * 8

SCRATCH = {
    "wk": ("sbuf", [128, _n[0]], "float32"),
    "IP": ("sbuf", [128, 1], "int32"), "M16": ("sbuf", [128, 16], "int32"), "UI": ("sbuf", [128, 16], "int32"),
    "I15": ("sbuf", [128, 1], "int32"), "I3": ("sbuf", [128, 1], "int32"), "ZI": ("sbuf", [128, 16], "int32"),
    "PLACE": ("sbuf", [128, C], "float32"), "LOF": ("sbuf", [128, C], "float32"), "YO": ("sbuf", [128, C], "float32"),
    "UO": ("sbuf", [128, 16], "uint16"), "LB1": ("sbuf", [128, 16], "uint16"), "LB2": ("sbuf", [128, 8], "uint16"),
    "LC": ("sbuf", [128, 16], "uint16"), "LO": ("sbuf", [128, 16], "uint16"),
    "ONE": ("sbuf", [128, 516], "bfloat16"), "EB": ("sbuf", [128, 516], "bfloat16"), "EB2": ("sbuf", [128, 516], "bfloat16"),
    "UT": ("sbuf", [128, 512], "bfloat16"), "VT": ("sbuf", [128, 512], "bfloat16"), "BT": ("sbuf", [128, 512], "bfloat16"),
    "ZT": ("sbuf", [128, 4 * C], "bfloat16"), "YS": ("sbuf", [128, 4 * C], "bfloat16"), "AW": ("sbuf", [128, 4 * AWID], "bfloat16"),
    "FH": ("sbuf", [128, 2 * C], "bfloat16"), "AS": ("sbuf", [128, 2 * C], "bfloat16"),
}
for _name, _w in (("E", 512), ("EH", 256), ("QU", 128), ("UC", 256), ("QV", 128), ("W", 512), ("QZ", 256), ("QM0", 128), ("QM1", 128),
                  ("QM2", 128), ("QX0", AWID), ("QX1", AWID), ("QX2", AWID), ("QX3", C), ("QB0", 128), ("QB1", 128), ("QB2", 128)):
    SCRATCH[_name + "c"] = ("sbuf", [128, _w], "float8_e4m3fn_x4")
    SCRATCH[_name + "p"] = ("sbuf", [128, _w], "uint8")
for _t in range(R + 1):
    SCRATCH["XW%d" % _t] = ("sbuf", [128, XWID], "bfloat16")
for _b in range(8):
    SCRATCH["p%d" % _b] = ("psum", [128, 512], "float32")
LOADS = ["xm", "xa", "xb", "u", "v", "wc", "ws"]
STORES = ["oc", "os0", "os1", "os2", "os3", "y0", "y1", "lo"]
SEMAPHORES = ["cv", "cs", "ct", "cg"] + ["d_" + n for n in LOADS + STORES] + ["arr%d" % t for t in range(R)] + ["loc%d" % t for t in range(R)]


def rank_program(g, core, T, topo):
    rank = T.rank_of(core)
    if rank is None:
        return
    V, S, P, Y = g.vector, g.scalar, g.tensor, g.sync
    queue = {"v": V, "s": S, "t": P, "g": g, "y": Y}
    count = {}
    waited = {}
    known = {q: {} for q in queue}
    behind = {}
    log = {}

    def need(q, name, a, b, write, out):
        for x in log.get(name, ()):
            if x[0] < b and a < x[1]:
                if x[3] != q:
                    if write or x[2] or name[0] == "p" and name[1:].isdigit():
                        out.append(x[4])
                elif x[2] and not write:
                    out.append(x[4])

    def note(q, name, a, b, write, ev):
        rows = log.setdefault(name, [])
        if write:
            rows[:] = [x for x in rows if not (a <= x[0] and x[1] <= b)]
        rows.append((a, b, write, q, ev))

    def wait(q, ev):
        sem, val = ev
        if known[q].get(sem, 0) >= val:
            return
        queue[q].wait_ge(T.sem[sem], val)
        waited[sem] = max(waited.get(sem, 0), val)
        for s, n in list(behind.get(ev, {}).items()) + [(sem, val)]:
            known[q][s] = max(known[q].get(s, 0), n)

    def pre(q, rd, wr):
        evs = []
        for r in rd:
            need(q, r[0], r[1], r[2], False, evs)
        for r in wr:
            need(q, r[0], r[1], r[2], True, evs)
        most = {}
        for s, n in evs:
            most[s] = max(most.get(s, 0), n)
        for s in sorted(most, key=lambda s: (s == "c" + q, s)):
            wait(q, (s, most[s]))

    def emit(q, fn, rd, wr):
        pre(q, rd, wr)
        sem = "c" + q
        count[sem] = count.get(sem, 0) + 1
        fn().then_inc(T.sem[sem], 1)
        ev = (sem, count[sem])
        behind[ev] = dict(known[q])
        for r in rd:
            note(q, r[0], r[1], r[2], False, ev)
        for r in wr:
            note(q, r[0], r[1], r[2], True, ev)

    def dma(q, name, out, in_, rd, wr):
        pre(q, rd, wr)
        sem = "d_" + name
        count[sem] = 16
        queue[q].dma_start(out, in_).then_inc(T.sem[sem], 16)
        ev = (sem, 16)
        behind[ev] = dict(known[q])
        for r in rd:
            note(sem, r[0], r[1], r[2], False, ev)
        for r in wr:
            note(sem, r[0], r[1], r[2], True, ev)

    def reg(n):
        return ("wk", WORK[n][0], WORK[n][0] + WORK[n][1])

    def cut(n, a, b):
        return ("wk", WORK[n][0] + a, WORK[n][0] + b)

    def norm(x):
        return reg(x) if isinstance(x, str) else x

    def ap(x):
        return T[x[0]][:, x[1]:x[2]]

    def lanes(name, a, b):
        return [(name + "#%d" % i, a, b) for i in range(4)]

    def ts(out, in0, s1, s2, op0, op1=None):
        out, in0 = norm(out), norm(in0)
        rd = [in0]
        sc = []
        for s in (s1, s2):
            if isinstance(s, (str, tuple)):
                s = norm(s)
                rd.append(s)
                s = ap(s)
            sc.append(s)
        if op1 is None:
            emit("v", lambda: V.tensor_scalar(ap(out), ap(in0), sc[0], None, op0), rd, [out])
        else:
            emit("v", lambda: V.tensor_scalar(ap(out), ap(in0), sc[0], sc[1], op0, op1), rd, [out])

    def tt(out, x, y, op):
        out, x, y = norm(out), norm(x), norm(y)
        emit("v", lambda: V.tensor_tensor(ap(out), ap(x), ap(y), op), [x, y], [out])

    def act(out, x, scale, bias, func=F.Identity):
        out, x = norm(out), norm(x)
        rd = [x]
        if isinstance(bias, (str, tuple)):
            bias = norm(bias)
            rd.append(bias)
            bias = ap(bias)
        emit("s", lambda: S.activation(ap(out), ap(x), func, bias=bias, scale=scale), rd, [out])

    def quant(dst, a, n, src, sa, rd):
        emit("v", lambda: V.quantize_mx(T[dst + "c"][:, a:a + n], T[dst + "p"][:, a:a + n], T[src][:, sa:sa + 4 * n]), rd, [(dst, a, a + n)])

    def mm(bank, n, st, sa, mv, ma, start=True, stop=True):
        emit("t", lambda: P.matmul_mx(T["p%d" % bank][:, 0:n], T[st + "c"][:, sa:sa + 128], T[st + "p"][:, sa:sa + 128],
                                      T[mv + "c"][:, ma:ma + n], T[mv + "p"][:, ma:ma + n], start, stop),
             [(st, sa, sa + 128), (mv, ma, ma + n)], [("p%d" % bank, 0, 512)])

    def fill(name, a, b, val, wr=None):
        emit("v", lambda: V.memset(T[name][:, a:b], val), [], wr or [(name, a, b)])

    def psum_copy(q, out, oa, bank, a, b, scale):
        rd, wr = [("p%d" % bank, 0, 512)], [(out, oa, oa + b - a)]
        src, to = T["p%d" % bank][:, a:b], T[out][:, oa:oa + b - a]
        if q == "v":
            emit("v", lambda: V.tensor_scalar(to, src, scale, None, A.mult), rd, wr)
        else:
            emit("s", lambda: S.activation(to, src, F.Copy, scale=scale), rd, wr)

    def gather(q, out, win, off, rd, wr):
        if q == "v":
            emit("v", lambda: V.tensor_copy(out, win.indirect(off)), rd, wr)
        else:
            emit("s", lambda: S.activation(out, win.indirect(off), F.Copy), rd, wr)

    for name, a, b in (("xm", 64, 192), ("xa", 0, 64), ("xb", 192, 256)):
        dma("y", name, T.XW0[:, XB + 4 * a:XB + 4 * b], T.x[:, 4 * a:4 * b], [], lanes("XW0", a, b))
    dma("s", "u", T.UT[:, 0:512], T.u[:, 0:512], [], [("UT", 0, 512)])
    dma("y", "wc", T.Wc[:, 0:512].bitcast(dt.uint8), T.wc[:, 0:2048], [], [("W", 0, 512)])
    dma("y", "ws", T.Wp[:, 0:512], T.ws[:, 0:512], [], [("Ws", 0, 512)])
    dma("y", "v", T.VT[:, 0:512], T.v[:, 0:512], [], [("VT", 0, 512)])

    fill("ONE", 0, 516, 32.0)
    emit("g", lambda: g.iota(T.UI[:, 0:16], [[1, 2], [16, 8]], 0, 0), [], [("UI", 0, 16)])
    emit("g", lambda: g.iota(T.IP[:, 0:1], [[1, 1]], 0, 1), [], [("IP", 0, 1)])
    emit("g", lambda: g.iota(T.M16[:, 0:16], [[16, 16]], 0, 0), [], [("M16", 0, 16)])
    emit("g", lambda: g.affine_select(T.EB[:, 0:516], T.ONE[:, 0:516], [[-1, 516]], A.is_equal, 0.0, 4, 4), [("ONE", 0, 516)], [("EB", 0, 516)])
    emit("g", lambda: g.iota(T.PLACE[:, 0:C], [[1, C]], 0, 0, allow_small_or_imprecise_dtypes=True), [], [("PLACE", 0, C)])
    fill("XW0", 0, XB, 0.0, lanes("XW0", -PAD, 0))
    fill("wk", WORK["NEG"][0], WORK["NEG"][0] + 72, -1.0e29)
    fill("wk", WORK["MK"][0] + 17, WORK["MK"][0] + 18, 256.0)
    fill("BT", 384, 512, 0.0, lanes("BT", 96, 128))
    emit("v", lambda: V.tensor_copy(T.UO[:, 0:16], T.UI[:, 0:16]), [("UI", 0, 16)], [("UO", 0, 16)])
    ts(("I15", 0, 1), ("IP", 0, 1), 15, None, A.bitwise_and)
    ts(("I3", 0, 1), ("IP", 0, 1), 3, None, A.bitwise_and)
    emit("v", lambda: V.tensor_copy(ap(reg("S15")), T.I15[:, 0:1]), [("I15", 0, 1)], [reg("S15")])
    emit("v", lambda: V.tensor_copy(ap(reg("T3")), T.I3[:, 0:1]), [("I3", 0, 1)], [reg("T3")])
    ts("J", ("M16", 0, 16), "S15", None, A.add)
    ts(cut("MC", 65, 66), "T3", 382.0, None, A.add)
    ts("QT", "T3", -0.25, 0.5, A.mult, A.add)
    ts("I1", "J", "T3", 322.0, A.subtract, A.add)
    ts("ZQ", cut("J", 0, 8), "T3", 258.0, A.subtract, A.add)
    fill("XW0", XB + 4 * C, XWID, 0.0, lanes("XW0", C, C + PAD))
    for i in (1, 2):
        for a in (0, XB + 4 * C):
            j = -PAD if a == 0 else C
            emit("s", lambda: S.activation(T["XW%d" % i][:, a:a + XB], T.XW0[:, 0:XB], F.Copy), lanes("XW0", -PAD, 0), lanes("XW%d" % i, j, j + PAD))
    quant("QU", 0, 128, "UT", 0, [("UT", 0, 512)])
    quant("QM0", 0, 128, "XW0", XB + 4 * 64, lanes("XW0", 64, 192))
    emit("s", lambda: S.activation(T.UCp[:, 0:256], T.QUp[:, 0:128].indirect(T.UO[:, 0:16]), F.Copy), [("QU", 0, 128), ("UO", 0, 16)], [("UCs", 0, 256)])
    act(("EB2", 0, 516), ("EB", 0, 516), 1.0 / 64, 0.0)
    emit("v", lambda: V.tensor_copy(T.UCc[:, 0:256].bitcast(dt.uint32), T.QUc[:, 0:128].bitcast(dt.uint32).indirect(T.UO[:, 0:16])),
         [("QU", 0, 128), ("UO", 0, 16)], [("UC", 0, 256)])

    dst = T.cores[(rank - 1) % len(T.cores)]
    rid, pid = topo.addr(dst)[:2]
    mask = topo.mask(core, dst)
    lands = 2 * len(topo.engines(core, dst))

    def e_tile(b):
        return ("E", 128 * b, 1.0 / 64) if b < 2 else ("EH", 128 * b - 256, 1.0)

    for t in range(R):
        last = t == R - 1
        XW, QX, QM, QB = "XW%d" % t, "QX%d" % t, "QM%d" % t, "QB%d" % t
        NX = "XW%d" % (t + 1)
        if t == 0:
            pre("t", [("UCs", 0, 256)], [])
        else:
            quant(QM, 0, 128, XW, XB + 4 * 64, lanes(XW, 64, 192))
        mm(5, 128, "UC", 128, QM, 0)
        mm(4, 128, "UC", 0, QM, 0)
        if t > 0:
            for a in (0, 192):
                gather("v", T[XW][:, XB + 4 * a + 1:XB + 4 * a + 256:4], T.YS[:, C:2 * C], T.LO[:, a // 16:a // 16 + 4],
                       [("YS", C, 2 * C), ("LO", 0, 16)], [(XW + "#1", a, a + 64)])
        emit("v", lambda: V.tensor_tensor_scan(ap(cut("PK", 0, 17)), T.p5[:, 0:17], ap(cut("NEG", 0, 17)), -1.0e29, A.max, A.max),
             [("p5", 0, 512), reg("NEG")], [cut("PK", 0, 17)])
        emit("v", lambda: V.tensor_tensor_scan(ap(cut("PC", 0, 65)), T.p4[:, 32:97], ap(cut("NEG", 0, 65)), -1.0e29, A.max, A.max),
             [("p4", 0, 512), reg("NEG")], [cut("PC", 0, 65)])
        ts(cut("MK", 0, 17), cut("PK", 0, 17), cut("PK", 16, 17), 4.0, A.is_lt, A.mult)
        ts(cut("MC", 0, 65), cut("PC", 0, 65), cut("PC", 64, 65), 4.0, A.is_lt, A.mult)
        emit("v", lambda: V.tensor_reduce(ap(reg("K4")), ap(cut("MK", 0, 18)), AxisListType.X, A.add), [cut("MK", 0, 18)], [reg("K4")])
        emit("v", lambda: V.tensor_reduce(ap(reg("C4")), ap(cut("MC", 0, 66)), AxisListType.X, A.add), [cut("MC", 0, 66)], [reg("C4")])
        act("k2", "K4", 0.5, 0.0)
        act("c", "C4", 0.25, "QT")
        ts("mk", "ZQ", "K4", -2.0, A.is_gt, A.mult)
        ts(("LB1", 0, 16), "I1", "C4", "K4", A.add, A.subtract)
        ts("f", "K4", 2.0, "C4", A.mult, A.is_lt)
        ts("w1", "mk", "K4", "K4", A.mult, A.add)
        act("cpk", "K4", 0.25, "c")
        ts("m", "mk", "f", 1.0, A.mult, A.add)
        tt("r0", "ZQ", "w1", A.subtract)
        ts("x2", "J", "c", "k2", A.is_ge, A.mult)
        tt("r", "r0", "m", A.mult)
        ts("x3", "J", "cpk", "k2", A.is_ge, A.mult)
        ts(("LB2", 0, 8), "r", "C4", float(XB), A.add, A.add)
        tt("y2", "x2", "x3", A.subtract)
        allx = lanes(XW, -PAD, C + PAD)
        gather("s", T.BT[:, 0:256], T[XW][:, 0:XWID], T.LB1[:, 0:16], allx + [("LB1", 0, 16)], lanes("BT", 0, 64))
        gather("v", T.BT[:, 256:384], T[XW][:, 0:XWID], T.LB2[:, 0:8], allx + [("LB2", 0, 8)], lanes("BT", 64, 96))
        quant(QB, 0, 128, "BT", 0, lanes("BT", 0, 128))
        pre("g", [(QB, 0, 96)], [])
        g.remote_dma(out_ap=T[QX + "c"][:, C:AWID].bitcast(dt.uint8), in_ap=T[QB + "c"][:, 0:K].bitcast(dt.uint8),
                     remote_sem=T.sem["arr%d" % t], local_sem=T.sem["loc%d" % t], pid=pid, routing_id=rid, dma_engine_mask=mask)
        g.remote_dma(out_ap=T[QX + "p"][:, C:AWID], in_ap=T[QB + "p"][:, 0:K],
                     remote_sem=T.sem["arr%d" % t], local_sem=T.sem["loc%d" % t], pid=pid, routing_id=rid, dma_engine_mask=mask)
        count["arr%d" % t] = lands
        count["loc%d" % t] = lands
        note("remote", QX, C, AWID, True, ("arr%d" % t, lands))
        act("n3", "K4", -0.25, "c")
        act("c2", "c", 2.0, -256.5)
        act("rl", "k2", -1.0, "c", F.Relu)
        act("n2", "cpk", -1.0, 256.0)
        act("bn", "n3", BIG, 0.0)
        act("kb", "K4", 0.25, -128.25)
        act("Rr", "J", -1.0, "c2")
        act("x1", "J", -BIG, "bn", F.Relu)
        act("l3", "J", 0.5, "kb")
        act("tau", "cpk", 2.0, -256.0)
        act("rho", "rl", 1.0, "k2")
        act("nkw", "K4", -0.5, -255.5)
        act("bt", "tau", -BIG, BIG)
        act("br", "rho", BIG, 0.0)
        act("nch", "c", -1.0, 0.5)
        act("o2", "J", BIG, "bt", F.Relu)
        act("o1", "J", -BIG, "br", F.Relu)
        act("w", "J", 1.0, "nkw")
        act("ae", "J", 1.0, "nch", F.Abs)
        act("nk", "K4", -0.25, 0.0)
        act("k", "K4", 0.25, 0.0)
        act("ay", "ae", 1.0, "nk", F.Abs)
        act("km1", "K4", 0.25, -1.0)
        quant(QX, 0, C, XW, XB, lanes(XW, 0, C))
        if t == 0:
            for b in (0, 1):
                quant("E", 128 * b, 128, "EB", 4 - b, [("EB", 0, 516)])
            for b in (2, 3):
                quant("EH", 128 * b - 256, 128, "EB2", 4 - b, [("EB2", 0, 516)])
        for b in range(4):
            e, ea, sc = e_tile(b)
            mm(b, C, e, ea, QX, 0)
            psum_copy("s", "AW", AWID * b, b, 0, C, sc)
            if b < 2:
                emit("g", lambda: g.affine_select(T.FH[:, C * b:C * b + C], T.AW[:, AWID * b:AWID * b + C], [[1, C]], A.is_ge, 0.0, 0, 0),
                     [("AW", AWID * b, AWID * b + C)], [("FH", C * b, C * b + C)])
        if t == 0:
            ts("J1", "J", -1.0, None, A.add)
            ts("H1", "J", 0.25, -0.375, A.mult, A.add)
        ts("a", "n2", "n3", None, A.min)
        tt("y1", "Rr", "x1", A.add)
        ts("l2", "J1", "a", 1.0 / 3, A.subtract, A.mult)
        ts("l4", "J", "k2", "a", A.subtract, A.subtract)
        tt("v", "y1", "y2", A.add)
        tt("m1", "l2", "l3", A.max)
        tt("m2", "l4", "H1", A.max)
        ts("v0", "v", -0.5, BIG, A.is_gt, A.mult)
        ts("v1", "v", -255.75, BIG, A.is_lt, A.mult)
        tt(("ZI", 0, 16), "m1", "m2", A.max)
        z = ("ZI", 0, 16)
        tt("v2", "v0", "v1", A.add)
        tt("o3", "o1", "o2", A.add)
        ts("t2", z, "n2", None, A.min)
        tt("v3", "v2", "v", A.add)
        tt("o4", "o3", "w", A.add)
        ts("t3", z, "n3", None, A.min)
        tt("mn", "o4", "ay", A.min)
        ts("t1", z, "km1", 2.0, A.min, A.mult)
        tt("mm", "v3", "mn", A.min)
        tt("u", "t2", "t3", A.add)
        ts(("LC", 0, 16), "mm", 255.5, None, A.add)
        tt("N", "u", "t1", A.add)
        ts("zk", z, "k", 0.5, A.subtract, A.add)
        tt("I", "J", "N", A.subtract)
        ts("zl", z, "n2", 1.0, A.is_lt, A.add)
        ts("mo", "I", 2.0, 2.0, A.is_ge, A.mult)
        ts("ti", "I", -2.0, 1.0, A.mult, A.add)
        tt("xx", "mo", "zl", A.mult)
        ts("km", "mo", "k", None, A.mult)
        tt("gg", "ti", "xx", A.add)
        if t == 0:
            for b in (2, 3):
                quant("E", 128 * b, 128, "EB", 4 - b, [("EB", 0, 516)])
        for b in (0, 2, 1, 3):
            e, ea, sc = e_tile(b)
            mm(4 + b, 128, e, ea, QX, AWID - 128)
        for b in (2, 3):
            psum_copy("s", "AW", AWID * b + C, 4 + b, 128 - K, 128, 1.0)
        for b in (2, 3):
            gather("s", T.AS[:, C * b - 2 * C:C * b - C], T.AW[:, AWID * b:AWID * b + AWID], T.LC[:, 0:16],
                   [("AW", AWID * b, AWID * b + AWID), ("LC", 0, 16)], [("AS", C * b - 2 * C, C * b - C)])
        for b in (0, 1):
            psum_copy("v", "AW", AWID * b + C, 4 + b, 128 - K, 128, 1.0 / 64)
        for b in (0, 1):
            w = T.AW[:, AWID * b:AWID * b + AWID]
            emit("v", lambda: V.tensor_tensor(T.ZT[:, b:4 * C:4], w.indirect(T.LC[:, 0:16]), T.FH[:, C * b:C * b + C], A.add),
                 [("AW", AWID * b, AWID * b + AWID), ("FH", C * b, C * b + C), ("LC", 0, 16)], [("ZT#%d" % b, 0, C)])
        for b in (2, 3):
            emit("v", lambda: V.tensor_tensor(T.ZT[:, b:4 * C:4], T.AS[:, C * b - 2 * C:C * b - C], T["p%d" % b][:, 0:C], A.add),
                 [("AS", C * b - 2 * C, C * b - C), ("p%d" % b, 0, 512)], [("ZT#%d" % b, 0, C)])
        tt("D", "zk", "km", A.add)
        quant("QZ", 0, C, "ZT", 0, lanes("ZT", 0, C))
        for b in (0, 2, 1, 3):
            mm(4 + b, C, "E", 128 * b, QX, 0, True, False)
        if t == 0:
            pre("t", [("Ws", 0, 512)], [])
        for b in range(4):
            mm(4 + b, C, "W", 128 * b, "QZ", 0, False, True)
        tt("gD", "gg", "D", A.mult)
        ts(("LO", 0, 16), "gD", "c", -0.5, A.add, A.add)

        def page(q, b, a, n):
            gather(q, T[NX][:, XB + 4 * a + b:XB + 4 * a + 4 * n:4], T.YS[:, C * b:C * b + C], T.LO[:, a // 16:(a + n) // 16],
                   [("YS", C * b, C * b + C), ("LO", 0, 16)], [(NX + "#%d" % b, a, a + n)])
        for b in range(4):
            psum_copy("sv"[b % 2], "YS", C * b, 4 + b, 0, C, 0.03125)
        for b in range(4):
            page("sv"[b % 2], b, 0 if last else 64, C if last else 128)
        if not last:
            for b in (0, 2, 3):
                page("s", b, 0, 64)
                page("s", b, 192, 64)
    XW, QX = "XW%d" % R, "QX%d" % R
    quant("QV", 0, 128, "VT", 0, [("VT", 0, 512)])
    for h in range(2):
        quant(QX, 128 * h, 128, XW, XB + 512 * h, lanes(XW, 128 * h, 128 * h + 128))
    for h in range(2):
        mm(h, 128, "QV", 0, QX, 128 * h)
        psum_copy("v", "YO", 128 * h, h, 0, 128, 1.0)
    gather("s", T.LOF[:, 0:C], T.PLACE[:, 0:C], T.LO[:, 0:16], [("PLACE", 0, C), ("LO", 0, 16)], [("LOF", 0, C)])
    dma("y", "oc", T.oc[:, 0:4 * C], T[QX + "c"][:, 0:C].bitcast(dt.uint8), [(QX, 0, C)], [])
    dma("s", "lo", T.lo[:, 0:C], T.LOF[0:128:16, 0:C], [("LOF", 0, C)], [])
    for i in range(4):
        dma("yyss"[i], "os%d" % i, T.osc[4 * i:4 * i + 4, 0:C], T[QX + "p"][32 * i:32 * i + 4, 0:C], [(QX, 0, C)], [])
    for h in range(2):
        dma("y", "y%d" % h, T.y[:, 128 * h:128 * h + 128], T.YO[:, 128 * h:128 * h + 128], [("YO", 128 * h, 128 * h + 128)], [])
    for sem in sorted(count, key=lambda s: (s[0] == "d", s)):
        if waited.get(sem, 0) < count[sem]:
            wait("g", (sem, count[sem]))
